import numpy as np
import ml_dtypes


def mxq(x, axis, fmt="e4m3"):
    dtype, down = {"e4m3": (ml_dtypes.float8_e4m3fn, 7), "e5m2": (ml_dtypes.float8_e5m2, 14)}[fmt]
    v = np.moveaxis(np.asarray(x, np.float32).astype(ml_dtypes.bfloat16).astype(np.float64), axis, -1)
    blocks = v.reshape(v.shape[:-1] + (-1, 32))
    amax = np.abs(blocks).max(-1, keepdims=True)
    byte = np.maximum(np.where(amax > 0, np.frexp(amax)[1] - 1 + 127, 0) - down, 1)
    scale = np.exp2(byte - 127.0)
    codes = (blocks / scale).astype(np.float32).astype(dtype).astype(np.float64)
    return np.moveaxis((codes * scale).reshape(v.shape), -1, axis)


WIDE = False


def mx_kscale(k):
    if not WIDE:
        return np.ones(k)
    levels = np.array([10, -10, 5, -5, 0])
    if k % 512:
        return np.exp2(np.random.permutation(np.resize(levels, k // 32))).repeat(32)
    a = np.empty((k // 512, 16))
    for p in range(k // 512):
        a[p, :8] = np.random.permutation(np.resize(levels, 8))
        for g in range(8):
            far = levels[np.abs(levels - a[p, g]) >= 10]
            a[p, g + 8] = far[np.random.randint(len(far))]
    return np.exp2(a.ravel()).repeat(32)


def f64(x):
    return np.asarray(x).astype(np.float64)


def striped(idx):
    return np.tile(idx.reshape(-1, 16).T, (8, 1)).astype(np.uint16)


def unstriped(offs):
    return offs[:16].T.reshape(-1).astype(np.int64)


E2M1 = np.array([0.0, 0.5, 1.0, 1.5, 2.0, 3.0, 4.0, 6.0, -0.0, -0.5, -1.0, -1.5, -2.0, -3.0, -4.0, -6.0])


def pack_weight(w, fmt):
    k, n = w.shape
    w = f64(np.asarray(w, np.float32).astype(ml_dtypes.bfloat16)).reshape(k // 32, 32, n)
    amax = np.abs(w).max(1)
    if fmt == "e4m3":
        byte = np.frexp(amax)[1] - 1 + 127 - 7
    else:
        mant, ex = np.frexp(amax / 6.0)
        byte = np.where(mant > 0.5, ex, ex - 1) + 127
    byte = np.clip(np.where(amax > 0, byte, 1), 1, 254)
    scaled = (w * np.exp2(127.0 - byte)[:, None, :]).reshape(k, n).astype(np.float32)
    by_word = np.ascontiguousarray(scaled.reshape(k // 512, 128, 4, n).transpose(0, 1, 3, 2))
    if fmt == "e4m3":
        words = by_word.astype(ml_dtypes.float8_e4m3fn).view(np.uint8)
    else:
        c = by_word.astype(ml_dtypes.float4_e2m1fn).view(np.uint8) & 0xF
        words = (c[..., 0::2] | (c[..., 1::2] << 4)).reshape(k // 512, 128, 2 * n)
    return np.ascontiguousarray(words), np.ascontiguousarray(byte.astype(np.uint8).reshape(k // 512, 16, n))


def unpack_weight(words, scales, fmt):
    g, _, n = scales.shape
    words = np.ascontiguousarray(words).reshape(g, 128, n, -1)
    if fmt == "e4m3":
        vals = words.view(ml_dtypes.float8_e4m3fn).astype(np.float64)
    else:
        nib = np.empty((g, 128, n, 4), np.uint8)
        nib[..., 0::2] = words & 0xF
        nib[..., 1::2] = words >> 4
        vals = E2M1[nib]
    vals = vals * np.repeat(np.exp2(scales.astype(np.float64) - 127.0), 8, axis=1)[..., None]
    return vals.transpose(0, 1, 3, 2).reshape(g * 512, n)


def gelu(v):
    return 0.5 * v * (1.0 + np.tanh(np.sqrt(2.0 / np.pi) * (v + 0.044715 * v**3)))


K, K2, H, N, T, T2, S = 1024, 512, 1024, 256, 4096, 2048, 1024

def setup_inputs():
    n = np.random.standard_normal
    s = mx_kscale(K)[:, None]
    s2 = mx_kscale(K2)[:, None]
    u = mx_kscale(H)[:, None]
    tab_words, tab_scales = pack_weight(n((K, T)) * s, "e4m3")
    tab2_words, tab2_scales = pack_weight(n((K2, T2)) * s2, "e4m3")
    w2_words, w2_scales = pack_weight(n((K2, H)) / np.sqrt(K2) / s2, "e2m1")
    w3_words, w3_scales = pack_weight(n((H, N)) / np.sqrt(H) / u, "e4m3")
    return {
        "tab_words": tab_words, "tab_scales": tab_scales,
        "tab2_words": tab2_words, "tab2_scales": tab2_scales,
        "offs": striped(np.random.permutation(T)[:S]),
        "offs2": striped(np.random.permutation(T2)[:S]),
        "w1": (n((K, H)) / np.sqrt(K) / s * u.T).astype(np.float32),
        "w2_words": w2_words, "w2_scales": w2_scales,
        "w3_words": w3_words, "w3_scales": w3_scales,
        "bias": (0.5 * n(N)).astype(np.float32),
    }

def reference(tab_words, tab_scales, tab2_words, tab2_scales, offs, offs2, w1, w2_words, w2_scales, w3_words, w3_scales, bias):
    v = unpack_weight(tab_words, tab_scales, "e4m3")[:, unstriped(offs)]
    v2 = unpack_weight(tab2_words, tab2_scales, "e4m3")[:, unstriped(offs2)]
    w1q = mxq(f64(w1), 0, "e4m3")
    w2 = unpack_weight(w2_words, w2_scales, "e2m1")
    w3 = unpack_weight(w3_words, w3_scales, "e4m3")
    a = w1q.T @ v
    b = w2.T @ v2
    h = a / (1.0 + np.square(b))
    hq = mxq(h, 0, "e4m3")
    y = w3.T @ hq
    return y + f64(bias)[:, None]

@@ -1,0 +1,207 @@
+from contextlib import ExitStack
+
+import concourse.mybir as mybir
+
+K, K2, H, N, T, T2, S = 1024, 512, 1024, 256, 4096, 2048, 1024
+FLOPS = 2 * S * (K * H + K2 * H + H * N)
+
+F32 = mybir.dt.float32
+BF16 = mybir.dt.bfloat16
+I32 = mybir.dt.int32
+U32 = mybir.dt.uint32
+U16 = mybir.dt.uint16
+U8 = mybir.dt.uint8
+FP8X4 = mybir.dt.float8_e4m3fn_x4
+FP4X4 = mybir.dt.float4_e2m1fn_x4
+ACT = mybir.ActivationFunctionType
+ALU = mybir.AluOpType
+
+P = 128
+PACK = 4
+PASS = P * PACK
+TOK = 128
+GROUPS = H // PASS
+BLOCKS = S // TOK
+
+
+def tile_list_damped_grasp_scores_kernel(tc, tab_words, tab_scales, tab2_words, tab2_scales, offs, offs2, w1,
+                                                  w2_words, w2_scales, w3_words, w3_scales, bias, out):
+    nc = tc.nc
+    with ExitStack() as ctx:
+        keep = ctx.enter_context(tc.tile_pool(name="keep", bufs=1))
+        ring = ctx.enter_context(tc.tile_pool(name="ring", bufs=3))
+        psum_a = ctx.enter_context(tc.psum_pool(name="psum_a", bufs=4))
+        psum_b = ctx.enter_context(tc.psum_pool(name="psum_b", bufs=2))
+        psum_y = ctx.enter_context(tc.psum_pool(name="psum_y", bufs=2))
+
+        def held(shape, dtype, name):
+            return keep.tile(shape, dtype, name=name, align_bytes=64)
+
+        list1 = keep.tile([P, S // 16], U16, name="list1")
+        list2 = keep.tile([P, S // 16], U16, name="list2")
+        v_window = [held([P, T], I32, "v_window%d" % a) for a in range(K // PASS)]
+        v_scale_window = held([P, T // 4], I32, "v_scale_window")
+        u_window = held([P, T2], I32, "u_window")
+        u_scale_window = held([P, T2 // 4], I32, "u_scale_window")
+        w2_raw = held([P, H // 2], I32, "w2_raw")
+        w2_scale_raw = held([P, H // 4], I32, "w2_scale_raw")
+        w3_codes = held([P, GROUPS, N], I32, "w3_codes")
+        w3_scale = held([P, GROUPS, N // 4], I32, "w3_scale")
+        bias_sb = held([P, N // P], F32, "bias_sb")
+        w1_raw = [[held([P, PACK, PASS], F32, "w1_raw%d%d" % (g, a)) for a in range(K // PASS)] for g in range(GROUPS)]
+
+        warm = held([P, 2], F32, "warm")
+        nc.vector.memset(w2_scale_raw[:], 0)
+        nc.vector.memset(u_scale_window[:], 0)
+        nc.vector.memset(warm[:, 0:1], 1.0)
+        nc.vector.memset(v_scale_window[:], 0)
+        nc.vector.memset(w3_scale[:], 0)
+        nc.scalar.activation(warm[:, 1:2], warm[:, 0:1], ACT.Abs_reciprocal_sqrt)
+
+        def load_w1(g, a):
+            rows = w1[a * PASS:(a + 1) * PASS, g * PASS:(g + 1) * PASS]
+            nc.sync.dma_start(w1_raw[g][a][:], rows.rearrange("(p j) c -> p j c", j=PACK))
+
+        def words_of(packed):
+            return packed.rearrange("p n t -> p (n t)").bitcast(I32)
+
+        nc.sync.dma_start(list2[:], offs2)
+        nc.sync.dma_start(w2_raw[:], w2_words[0].bitcast(I32))
+        for q in range(4):
+            nc.sync.dma_start(w2_scale_raw[32 * q:32 * q + 4, :], w2_scales[0, 4 * q:4 * q + 4, :].bitcast(I32))
+        nc.sync.dma_start(u_window[:], words_of(tab2_words[0]))
+        for q in range(4):
+            nc.sync.dma_start(u_scale_window[32 * q:32 * q + 4, :], tab2_scales[0, 4 * q:4 * q + 4, :].bitcast(I32))
+        load_w1(0, 0)
+        nc.sync.dma_start(list1[:], offs)
+        for a in range(K // PASS):
+            for q in range(4):
+                nc.sync.dma_start(v_scale_window[32 * q + 4 * a:32 * q + 4 * a + 4, :],
+                                  tab_scales[a, 4 * q:4 * q + 4, :].bitcast(I32))
+        load_w1(0, 1)
+        for a in range(K // PASS):
+            nc.sync.dma_start(v_window[a][:], words_of(tab_words[a]))
+        load_w1(1, 0)
+        load_w1(1, 1)
+        nc.sync.dma_start(w3_codes[:], w3_words.rearrange("a p n t -> p a (n t)").bitcast(I32))
+        for q in range(4):
+            nc.sync.dma_start(w3_scale[32 * q:32 * q + 4, :, :],
+                              w3_scales[:, 4 * q:4 * q + 4, :].rearrange("a r n -> r a n").bitcast(I32))
+        with nc.allow_non_contiguous_dma(reason="one bias value to a partition"):
+            nc.sync.dma_start(bias_sb[:], bias.rearrange("(c p) -> p c", p=P))
+
+        w2_codes = held([P, 2 * H], U8, "w2_codes")
+        w2_scale = held([P, H], U8, "w2_scale")
+        nc.vector.tensor_copy(w2_codes[:].bitcast(U16).rearrange("p (g t m) -> p g t m", g=GROUPS, t=PACK),
+                              w2_raw[:].bitcast(U16).rearrange("p (g m t) -> p g t m", g=GROUPS, t=PACK))
+        nc.vector.tensor_copy(w2_scale[:].rearrange("p (g t m) -> p g t m", g=GROUPS, t=PACK),
+                              w2_scale_raw[:].bitcast(U8).rearrange("p (g m t) -> p g t m", g=GROUPS, t=PACK))
+
+        def gather(dst, window, offsets, lo, hi):
+            nc.vector.tensor_copy(dst[:, lo:hi], window.indirect(offsets[:, lo // 16:hi // 16]))
+
+        u_codes = held([P, S], U32, "u_codes")
+        u_scale = held([P, S], U8, "u_scale")
+        for lo, hi in ((0, 256), (256, 512), (512, 1024)):
+            gather(u_codes, u_window[:].bitcast(U32), list2, lo, hi)
+            gather(u_scale, u_scale_window[:].bitcast(U8), list2, lo, hi)
+
+        damp = held([P, GROUPS, S * PACK], F32, "damp")
+        span = 2 * TOK * PACK
+        for g in range(GROUPS):
+            for pair in range(BLOCKS // 2):
+                squared = ring.tile([P, span], F32, name="squared")
+                for half in range(2):
+                    cols = slice((2 * pair + half) * TOK, (2 * pair + half + 1) * TOK)
+                    b_bank = psum_b.tile([P, PACK, TOK], F32, name="b_bank")
+                    for t in range(PACK):
+                        m0 = g * PASS + t * P
+                        nc.tensor.matmul_mx(out=b_bank[:, t, :], lhsT=w2_codes[:, 2 * m0:2 * (m0 + P)].bitcast(FP4X4),
+                                            lhsT_scale=w2_scale[:, m0:m0 + P], rhs=u_codes[:, cols].bitcast(FP8X4),
+                                            rhs_scale=u_scale[:, cols], start=True, stop=True)
+                    nc.scalar.activation(squared[:, half * PASS:(half + 1) * PASS].rearrange("p (n t) -> p n t", t=PACK),
+                                         b_bank[:].rearrange("p t n -> p n t"), ACT.Square)
+                root = ring.tile([P, span], F32, name="root")
+                nc.scalar.activation(root[:], squared[:], ACT.Abs_reciprocal_sqrt, bias=1.0)
+                nc.scalar.activation(damp[:, g, pair * span:(pair + 1) * span], root[:], ACT.Square)
+
+        w1_codes = held([P, GROUPS, K // PASS, PASS], U32, "w1_codes")
+        w1_scale = held([P, GROUPS, K // PASS, PASS], U8, "w1_scale")
+
+        def round_w1(g, a):
+            grouped = ring.tile([P, PACK, P, PACK], BF16, name="grouped", align_bytes=64)
+            nc.vector.tensor_copy(grouped[:].rearrange("p t m j -> p m t j"),
+                                  w1_raw[g][a][:].rearrange("p j (m t) -> p m t j", t=PACK))
+            return grouped
+
+        def quantize_w1(g, a, grouped):
+            nc.vector.quantize_mx(out=w1_codes[:, g, a, :].bitcast(FP8X4), scales=w1_scale[:, g, a, :],
+                                  in_=grouped[:].rearrange("p t m j -> p (t m j)"))
+
+        def prepare_w1(g):
+            rounded = [round_w1(g, a) for a in range(K // PASS)]
+            for a in range(K // PASS):
+                quantize_w1(g, a, rounded[a])
+
+        v_codes = [held([P, S], U32, "v_codes%d" % a) for a in range(K // PASS)]
+        v_scale = held([P, S], U8, "v_scale")
+        h_codes = held([P, GROUPS, S], U32, "h_codes")
+        h_scale = held([P, GROUPS, S], U8, "h_scale")
+
+        def damped(g, lo, hi):
+            h_bf = ring.tile([P, (hi - lo) * PACK], BF16, name="h_bf", align_bytes=64)
+            for n0 in range(lo, hi, TOK):
+                cols = slice(n0, n0 + TOK)
+                a_bank = psum_a.tile([P, PACK, TOK], F32, name="a_bank")
+                for t in range(PACK):
+                    m_cols = slice(t * P, (t + 1) * P)
+                    for a in range(K // PASS):
+                        nc.tensor.matmul_mx(out=a_bank[:, t, :], lhsT=w1_codes[:, g, a, m_cols].bitcast(FP8X4),
+                                            lhsT_scale=w1_scale[:, g, a, m_cols],
+                                            rhs=v_codes[a][:, cols].bitcast(FP8X4), rhs_scale=v_scale[4 * a:P, cols],
+                                            start=(a == 0), stop=(a == K // PASS - 1))
+                nc.vector.tensor_tensor(
+                    h_bf[:, (n0 - lo) * PACK:(n0 - lo + TOK) * PACK].rearrange("p (n t) -> p n t", t=PACK),
+                    a_bank[:].rearrange("p t n -> p n t"),
+                    damp[:, g, n0 * PACK:(n0 + TOK) * PACK].rearrange("p (n t) -> p n t", t=PACK), ALU.mult)
+            return h_bf
+
+        def quantize_h(g, lo, hi, h_bf):
+            nc.vector.quantize_mx(out=h_codes[:, g, lo:hi].bitcast(FP8X4), scales=h_scale[:, g, lo:hi], in_=h_bf[:])
+
+        def scores(lo, hi):
+            y_bank = psum_y.tile([P, N // P, hi - lo], F32, name="y_bank")
+            y_sb = ring.tile([P, N // P, hi - lo], F32, name="y_sb")
+            for c in range(N // P):
+                for g in range(GROUPS):
+                    nc.tensor.matmul_mx(out=y_bank[:, c, :], lhsT=w3_codes[:, g, c * P:(c + 1) * P].bitcast(FP8X4),
+                                        lhsT_scale=w3_scale[:, g, :].bitcast(U8)[:, c * P:(c + 1) * P],
+                                        rhs=h_codes[:, g, lo:hi].bitcast(FP8X4), rhs_scale=h_scale[:, g, lo:hi],
+                                        start=(g == 0), stop=(g == GROUPS - 1))
+            for c in range(N // P):
+                nc.scalar.activation(y_sb[:, c, :], y_bank[:, c, :], ACT.Identity, bias=bias_sb[:, c:c + 1])
+            nc.sync.dma_start(out[:, lo:hi].rearrange("(c p) n -> p c n", p=P), y_sb[:])
+
+        prepare_w1(0)
+        halves = ((0, S // 2), (S // 2, S))
+        for lo, hi in halves:
+            gather(v_scale, v_scale_window[:].bitcast(U8), list1, lo, hi)
+        for lo, hi in halves:
+            gather(v_codes[0], v_window[0][:].bitcast(U32), list1, lo, hi)
+        for lo, hi in halves:
+            gather(v_codes[1], v_window[1][:].bitcast(U32), list1, lo, hi)
+
+        chunks = ((0, 256), (256, 512), (512, 768), (768, 896), (896, 1024))
+        for g in range(GROUPS):
+            if g > 0:
+                prepare_w1(g)
+            pending = None
+            for lo, hi in chunks:
+                h_bf = damped(g, lo, hi)
+                if pending is not None:
+                    quantize_h(g, *pending)
+                    if g == GROUPS - 1:
+                        scores(pending[0], pending[1])
+                pending = (lo, hi, h_bf)
+            quantize_h(g, *pending)
+        scores(pending[0], pending[1])

@@ -22,6 +22,10 @@ PASS = P * PACK
 TOK = 128
 GROUPS = H // PASS
 BLOCKS = S // TOK
+BANKS = 4
+LATE = 768
+FIRST = 256
+ON_VECTOR = (0, 1)
 
 
 def tile_list_damped_grasp_scores_kernel(tc, tab_words, tab_scales, tab2_words, tab2_scales, offs, offs2, w1,
@@ -29,13 +33,12 @@ def tile_list_damped_grasp_scores_kernel(tc, tab_words, tab_scales, tab2_words, 
     nc = tc.nc
     with ExitStack() as ctx:
         keep = ctx.enter_context(tc.tile_pool(name="keep", bufs=1))
-        ring = ctx.enter_context(tc.tile_pool(name="ring", bufs=3))
-        psum_a = ctx.enter_context(tc.psum_pool(name="psum_a", bufs=4))
-        psum_b = ctx.enter_context(tc.psum_pool(name="psum_b", bufs=2))
-        psum_y = ctx.enter_context(tc.psum_pool(name="psum_y", bufs=2))
+        ring = ctx.enter_context(tc.tile_pool(name="ring", bufs=4))
+        psum_ab = ctx.enter_context(tc.psum_pool(name="psum_ab", bufs=BANKS))
+        psum_by = ctx.enter_context(tc.psum_pool(name="psum_by", bufs=3))
 
-        def held(shape, dtype, name):
-            return keep.tile(shape, dtype, name=name, align_bytes=64)
+        def held(shape, dtype, name, tag=None):
+            return keep.tile(shape, dtype, name=name, tag=tag or name, align_bytes=64)
 
         list1 = keep.tile([P, S // 16], U16, name="list1")
         list2 = keep.tile([P, S // 16], U16, name="list2")
@@ -51,12 +54,11 @@ def tile_list_damped_grasp_scores_kernel(tc, tab_words, tab_scales, tab2_words, 
         w1_raw = [[held([P, PACK, PASS], F32, "w1_raw%d%d" % (g, a)) for a in range(K // PASS)] for g in range(GROUPS)]
 
         warm = held([P, 2], F32, "warm")
-        nc.vector.memset(w2_scale_raw[:], 0)
         nc.vector.memset(u_scale_window[:], 0)
+        nc.vector.memset(w2_scale_raw[:], 0)
         nc.vector.memset(warm[:, 0:1], 1.0)
         nc.vector.memset(v_scale_window[:], 0)
         nc.vector.memset(w3_scale[:], 0)
-        nc.scalar.activation(warm[:, 1:2], warm[:, 0:1], ACT.Abs_reciprocal_sqrt)
 
         def load_w1(g, a):
             rows = w1[a * PASS:(a + 1) * PASS, g * PASS:(g + 1) * PASS]
@@ -66,19 +68,20 @@ def tile_list_damped_grasp_scores_kernel(tc, tab_words, tab_scales, tab2_words, 
             return packed.rearrange("p n t -> p (n t)").bitcast(I32)
 
         nc.sync.dma_start(list2[:], offs2)
-        nc.sync.dma_start(w2_raw[:], w2_words[0].bitcast(I32))
-        for q in range(4):
-            nc.sync.dma_start(w2_scale_raw[32 * q:32 * q + 4, :], w2_scales[0, 4 * q:4 * q + 4, :].bitcast(I32))
-        nc.sync.dma_start(u_window[:], words_of(tab2_words[0]))
         for q in range(4):
             nc.sync.dma_start(u_scale_window[32 * q:32 * q + 4, :], tab2_scales[0, 4 * q:4 * q + 4, :].bitcast(I32))
-        load_w1(0, 0)
-        nc.sync.dma_start(list1[:], offs)
+        nc.sync.dma_start(w2_raw[:], w2_words[0].bitcast(I32))
+        nc.sync.dma_start(u_window[:], words_of(tab2_words[0]))
+        for q in range(4):
+            nc.sync.dma_start(w2_scale_raw[32 * q:32 * q + 4, :], w2_scales[0, 4 * q:4 * q + 4, :].bitcast(I32))
+        nc.scalar.activation(warm[:, 1:2], warm[:, 0:1], ACT.Abs_reciprocal_sqrt)
         for a in range(K // PASS):
+            load_w1(0, a)
+            if a == 1:
+                nc.sync.dma_start(list1[:], offs)
             for q in range(4):
                 nc.sync.dma_start(v_scale_window[32 * q + 4 * a:32 * q + 4 * a + 4, :],
                                   tab_scales[a, 4 * q:4 * q + 4, :].bitcast(I32))
-        load_w1(0, 1)
         for a in range(K // PASS):
             nc.sync.dma_start(v_window[a][:], words_of(tab_words[a]))
         load_w1(1, 0)
@@ -90,87 +93,126 @@ def tile_list_damped_grasp_scores_kernel(tc, tab_words, tab_scales, tab2_words, 
         with nc.allow_non_contiguous_dma(reason="one bias value to a partition"):
             nc.sync.dma_start(bias_sb[:], bias.rearrange("(c p) -> p c", p=P))
 
-        w2_codes = held([P, 2 * H], U8, "w2_codes")
-        w2_scale = held([P, H], U8, "w2_scale")
-        nc.vector.tensor_copy(w2_codes[:].bitcast(U16).rearrange("p (g t m) -> p g t m", g=GROUPS, t=PACK),
-                              w2_raw[:].bitcast(U16).rearrange("p (g m t) -> p g t m", g=GROUPS, t=PACK))
-        nc.vector.tensor_copy(w2_scale[:].rearrange("p (g t m) -> p g t m", g=GROUPS, t=PACK),
-                              w2_scale_raw[:].bitcast(U8).rearrange("p (g m t) -> p g t m", g=GROUPS, t=PACK))
-
         def gather(dst, window, offsets, lo, hi):
             nc.vector.tensor_copy(dst[:, lo:hi], window.indirect(offsets[:, lo // 16:hi // 16]))
 
-        u_codes = held([P, S], U32, "u_codes")
+        w2_codes = held([P, 2 * H], U8, "w2_codes")
+        w2_scale = held([P, H], U8, "w2_scale")
         u_scale = held([P, S], U8, "u_scale")
-        for lo, hi in ((0, 256), (256, 512), (512, 1024)):
-            gather(u_codes, u_window[:].bitcast(U32), list2, lo, hi)
-            gather(u_scale, u_scale_window[:].bitcast(U8), list2, lo, hi)
+        gather(u_scale, u_scale_window[:].bitcast(U8), list2, 0, S)
+        nc.vector.tensor_copy(w2_codes[:].bitcast(U16).rearrange("p (g t m) -> p g t m", g=GROUPS, t=PACK),
+                              w2_raw[:].bitcast(U16).rearrange("p (g m t) -> p g t m", g=GROUPS, t=PACK))
+        u_first = held([P, FIRST], U32, "u_first")
+        gather(u_first, u_window[:].bitcast(U32), list2, 0, FIRST)
+        nc.vector.tensor_copy(w2_scale[:].rearrange("p (g t m) -> p g t m", g=GROUPS, t=PACK),
+                              w2_scale_raw[:].bitcast(U8).rearrange("p (g m t) -> p g t m", g=GROUPS, t=PACK))
+        u_rest = held([P, S], U32, "u_rest", tag="w2_scale_raw")
+        for lo, hi in ((FIRST, 2 * FIRST), (2 * FIRST, S)):
+            gather(u_rest, u_window[:].bitcast(U32), list2, lo, hi)
 
         damp = held([P, GROUPS, S * PACK], F32, "damp")
+
+        def square_b(g, n0):
+            cols = slice(n0, n0 + TOK)
+            b_bank = psum_by.tile([P, PACK, TOK], F32, name="b_bank", tag="bank")
+            for t in range(PACK):
+                m0 = g * PASS + t * P
+                nc.tensor.matmul_mx(out=b_bank[:, t, :], lhsT=w2_codes[:, 2 * m0:2 * (m0 + P)].bitcast(FP4X4),
+                                    lhsT_scale=w2_scale[:, m0:m0 + P], rhs=(u_first if n0 < FIRST else u_rest)[:, cols].bitcast(FP8X4),
+                                    rhs_scale=u_scale[:, cols], start=True, stop=True)
+            nc.scalar.activation(damp[:, g, n0 * PACK:(n0 + TOK) * PACK].rearrange("p (n t) -> p n t", t=PACK),
+                                 b_bank[:].rearrange("p t n -> p n t"), ACT.Square)
+
         span = 2 * TOK * PACK
-        for g in range(GROUPS):
-            for pair in range(BLOCKS // 2):
-                squared = ring.tile([P, span], F32, name="squared")
-                for half in range(2):
-                    cols = slice((2 * pair + half) * TOK, (2 * pair + half + 1) * TOK)
-                    b_bank = psum_b.tile([P, PACK, TOK], F32, name="b_bank")
-                    for t in range(PACK):
-                        m0 = g * PASS + t * P
-                        nc.tensor.matmul_mx(out=b_bank[:, t, :], lhsT=w2_codes[:, 2 * m0:2 * (m0 + P)].bitcast(FP4X4),
-                                            lhsT_scale=w2_scale[:, m0:m0 + P], rhs=u_codes[:, cols].bitcast(FP8X4),
-                                            rhs_scale=u_scale[:, cols], start=True, stop=True)
-                    nc.scalar.activation(squared[:, half * PASS:(half + 1) * PASS].rearrange("p (n t) -> p n t", t=PACK),
-                                         b_bank[:].rearrange("p t n -> p n t"), ACT.Square)
-                root = ring.tile([P, span], F32, name="root")
-                nc.scalar.activation(root[:], squared[:], ACT.Abs_reciprocal_sqrt, bias=1.0)
-                nc.scalar.activation(damp[:, g, pair * span:(pair + 1) * span], root[:], ACT.Square)
+        spans = [(g, i * span) for g in range(GROUPS) for i in range(BLOCKS // 2)]
+        roots = {}
+
+        early_roots = held([P, 5 * span], F32, "early_roots")
+
+        def root_of(i, dst):
+            g, c0 = spans[i]
+            roots[i] = dst
+            nc.scalar.activation(dst, damp[:, g, c0:c0 + span], ACT.Abs_reciprocal_sqrt, bias=1.0)
+
+        for n0 in range(0, S, TOK):
+            square_b(0, n0)
+        for i in range(4):
+            root_of(i, early_roots[:, i * span:(i + 1) * span])
+        for i in range(len(ON_VECTOR), 4):
+            nc.scalar.activation(damp[:, 0, i * span:(i + 1) * span], roots[i], ACT.Square)
+        for n0 in range(0, S, TOK):
+            square_b(1, n0)
+        root_of(4, early_roots[:, 4 * span:5 * span])
+
+        def square_root_on_vector(i):
+            g, c0 = spans[i]
+            nc.vector.tensor_tensor(early_damp[:, c0:c0 + span], roots[i], roots[i], ALU.mult)
 
         w1_codes = held([P, GROUPS, K // PASS, PASS], U32, "w1_codes")
         w1_scale = held([P, GROUPS, K // PASS, PASS], U8, "w1_scale")
 
         def round_w1(g, a):
-            grouped = ring.tile([P, PACK, P, PACK], BF16, name="grouped", align_bytes=64)
-            nc.vector.tensor_copy(grouped[:].rearrange("p t m j -> p m t j"),
-                                  w1_raw[g][a][:].rearrange("p j (m t) -> p m t j", t=PACK))
+            grouped = held([P, PACK, P, PACK], BF16, "grouped%d%d" % (g, a))
+            src = w1_raw[g][a][:].rearrange("p j (m t) -> p m t j", t=PACK)
+            dst = grouped[:].rearrange("p t m j -> p m t j")
+            if (g, a) in ((1, 0),):
+                for m0 in range(0, P, 32):
+                    nc.gpsimd.tensor_scalar(dst[:, m0:m0 + 32], src[:, m0:m0 + 32], 1.0, 0.0, ALU.mult, ALU.add)
+            elif (g, a) in ((1, 1),):
+                nc.scalar.copy(dst, src)
+            else:
+                nc.vector.tensor_copy(dst, src)
             return grouped
 
         def quantize_w1(g, a, grouped):
             nc.vector.quantize_mx(out=w1_codes[:, g, a, :].bitcast(FP8X4), scales=w1_scale[:, g, a, :],
                                   in_=grouped[:].rearrange("p t m j -> p (t m j)"))
 
-        def prepare_w1(g):
-            rounded = [round_w1(g, a) for a in range(K // PASS)]
-            for a in range(K // PASS):
-                quantize_w1(g, a, rounded[a])
-
         v_codes = [held([P, S], U32, "v_codes%d" % a) for a in range(K // PASS)]
         v_scale = held([P, S], U8, "v_scale")
         h_codes = held([P, GROUPS, S], U32, "h_codes")
         h_scale = held([P, GROUPS, S], U8, "h_scale")
 
-        def damped(g, lo, hi):
-            h_bf = ring.tile([P, (hi - lo) * PACK], BF16, name="h_bf", align_bytes=64)
-            for n0 in range(lo, hi, TOK):
-                cols = slice(n0, n0 + TOK)
-                a_bank = psum_a.tile([P, PACK, TOK], F32, name="a_bank")
-                for t in range(PACK):
-                    m_cols = slice(t * P, (t + 1) * P)
-                    for a in range(K // PASS):
-                        nc.tensor.matmul_mx(out=a_bank[:, t, :], lhsT=w1_codes[:, g, a, m_cols].bitcast(FP8X4),
-                                            lhsT_scale=w1_scale[:, g, a, m_cols],
-                                            rhs=v_codes[a][:, cols].bitcast(FP8X4), rhs_scale=v_scale[4 * a:P, cols],
-                                            start=(a == 0), stop=(a == K // PASS - 1))
-                nc.vector.tensor_tensor(
-                    h_bf[:, (n0 - lo) * PACK:(n0 - lo + TOK) * PACK].rearrange("p (n t) -> p n t", t=PACK),
-                    a_bank[:].rearrange("p t n -> p n t"),
-                    damp[:, g, n0 * PACK:(n0 + TOK) * PACK].rearrange("p (n t) -> p n t", t=PACK), ALU.mult)
-            return h_bf
+        def project(g, n0):
+            cols = slice(n0, n0 + TOK)
+            a_bank = psum_ab.tile([P, PACK, TOK], F32, name="a_bank", tag="bank")
+            for t in range(PACK):
+                m_cols = slice(t * P, (t + 1) * P)
+                for a in range(K // PASS):
+                    nc.tensor.matmul_mx(out=a_bank[:, t, :], lhsT=w1_codes[:, g, a, m_cols].bitcast(FP8X4),
+                                        lhsT_scale=w1_scale[:, g, a, m_cols],
+                                        rhs=v_codes[a][:, cols].bitcast(FP8X4), rhs_scale=v_scale[4 * a:P, cols],
+                                        start=(a == 0), stop=(a == K // PASS - 1))
+            a_banks[g, n0] = a_bank
 
-        def quantize_h(g, lo, hi, h_bf):
-            nc.vector.quantize_mx(out=h_codes[:, g, lo:hi].bitcast(FP8X4), scales=h_scale[:, g, lo:hi], in_=h_bf[:])
+        h_bf = held([P, GROUPS, S * PACK], BF16, "h_bf")
+        a_banks = {}
+        waiting = []
+
+        def release(g):
+            waiting.extend((g, n0) for n0 in range(0, S, TOK))
+            while waiting and len(a_banks) < BANKS:
+                project(*waiting.pop(0))
+
+        def h_part(g, lo, hi):
+            if g == 0 and lo >= LATE:
+                return h_late[:, (lo - LATE) * PACK:(hi - LATE) * PACK]
+            return h_bf[:, g, lo * PACK:hi * PACK]
+
+        def damped(g, n0):
+            cols = slice(n0 * PACK, (n0 + TOK) * PACK)
+            factor = early_damp[:, cols] if g == 0 and cols.stop <= len(ON_VECTOR) * span else damp[:, g, cols]
+            nc.vector.tensor_tensor(h_part(g, n0, n0 + TOK).rearrange("p (n t) -> p n t", t=PACK),
+                                    a_banks.pop((g, n0))[:].rearrange("p t n -> p n t"),
+                                    factor.rearrange("p (n t) -> p n t", t=PACK), ALU.mult)
+            if waiting:
+                project(*waiting.pop(0))
+
+        def quantize_h(g, lo, hi):
+            nc.vector.quantize_mx(out=h_codes[:, g, lo:hi].bitcast(FP8X4), scales=h_scale[:, g, lo:hi], in_=h_part(g, lo, hi))
 
         def scores(lo, hi):
-            y_bank = psum_y.tile([P, N // P, hi - lo], F32, name="y_bank")
+            y_bank = psum_by.tile([P, N // P, hi - lo], F32, name="y_bank", tag="bank")
             y_sb = ring.tile([P, N // P, hi - lo], F32, name="y_sb")
             for c in range(N // P):
                 for g in range(GROUPS):
@@ -182,26 +224,45 @@ def tile_list_damped_grasp_scores_kernel(tc, tab_words, tab_scales, tab2_words, 
                 nc.scalar.activation(y_sb[:, c, :], y_bank[:, c, :], ACT.Identity, bias=bias_sb[:, c:c + 1])
             nc.sync.dma_start(out[:, lo:hi].rearrange("(c p) n -> p c n", p=P), y_sb[:])
 
-        prepare_w1(0)
         halves = ((0, S // 2), (S // 2, S))
-        for lo, hi in halves:
-            gather(v_scale, v_scale_window[:].bitcast(U8), list1, lo, hi)
-        for lo, hi in halves:
-            gather(v_codes[0], v_window[0][:].bitcast(U32), list1, lo, hi)
+        rounded = [round_w1(0, a) for a in range(K // PASS)]
+        for a in range(K // PASS):
+            quantize_w1(0, a, rounded[a])
+        early_damp = held([P, len(ON_VECTOR) * span], F32, "early_damp", tag="grouped01")
+        early_damp = held([P, len(ON_VECTOR) * span], F32, "early_damp", tag="grouped01")
+        for i in ON_VECTOR:
+            square_root_on_vector(i)
+        gather(v_scale, v_scale_window[:].bitcast(U8), list1, 0, S)
+        gather(v_codes[0], v_window[0][:].bitcast(U32), list1, 0, S)
         for lo, hi in halves:
             gather(v_codes[1], v_window[1][:].bitcast(U32), list1, lo, hi)
 
+        release(0)
+        rounded = [round_w1(1, a) for a in range(K // PASS)]
+        late_roots = held([P, 3 * span], F32, "late_roots", tag="w1_raw11")
+        for i in range(5, 9):
+            if i < 8:
+                root_of(i, late_roots[:, (i - 5) * span:(i - 4) * span])
+            nc.scalar.activation(damp[:, 1, (i - 5) * span:(i - 4) * span], roots[i - 1], ACT.Square)
+        for n0 in range(0, 512, TOK):
+            damped(0, n0)
+        quantize_w1(1, 0, rounded[0])
+        damped(0, 512)
+        quantize_h(0, 0, 512)
+        damped(0, 640)
+        quantize_w1(1, 1, rounded[1])
+        h_late = held([P, 2 * TOK * PACK], BF16, "h_late", tag="grouped11")
+        release(1)
+        damped(0, 768)
+        quantize_h(0, 512, 768)
+        damped(0, 896)
+        damped(1, 0)
+        quantize_h(0, 768, 1024)
         chunks = ((0, 256), (256, 512), (512, 768), (768, 896), (896, 1024))
-        for g in range(GROUPS):
-            if g > 0:
-                prepare_w1(g)
-            pending = None
-            for lo, hi in chunks:
-                h_bf = damped(g, lo, hi)
-                if pending is not None:
-                    quantize_h(g, *pending)
-                    if g == GROUPS - 1:
-                        scores(pending[0], pending[1])
-                pending = (lo, hi, h_bf)
-            quantize_h(g, *pending)
-        scores(pending[0], pending[1])
+        done = 128
+        for lo, hi in chunks:
+            while done < min(hi + TOK, S):
+                damped(1, done)
+                done += TOK
+            quantize_h(1, lo, hi)
+            scores(lo, hi)

@@ -25,7 +25,7 @@ BLOCKS = S // TOK
 BANKS = 4
 LATE = 768
 FIRST = 256
-ON_VECTOR = (0, 1)
+ON_VECTOR = (0,)
 
 
 def tile_list_damped_grasp_scores_kernel(tc, tab_words, tab_scales, tab2_words, tab2_scales, offs, offs2, w1,
@@ -35,7 +35,7 @@ def tile_list_damped_grasp_scores_kernel(tc, tab_words, tab_scales, tab2_words, 
         keep = ctx.enter_context(tc.tile_pool(name="keep", bufs=1))
         ring = ctx.enter_context(tc.tile_pool(name="ring", bufs=4))
         psum_ab = ctx.enter_context(tc.psum_pool(name="psum_ab", bufs=BANKS))
-        psum_by = ctx.enter_context(tc.psum_pool(name="psum_by", bufs=3))
+        psum_by = ctx.enter_context(tc.psum_pool(name="psum_by", bufs=4))
 
         def held(shape, dtype, name, tag=None):
             return keep.tile(shape, dtype, name=name, tag=tag or name, align_bytes=64)
@@ -159,7 +159,8 @@ def tile_list_damped_grasp_scores_kernel(tc, tab_words, tab_scales, tab2_words, 
                 for m0 in range(0, P, 32):
                     nc.gpsimd.tensor_scalar(dst[:, m0:m0 + 32], src[:, m0:m0 + 32], 1.0, 0.0, ALU.mult, ALU.add)
             elif (g, a) in ((1, 1),):
-                nc.scalar.copy(dst, src)
+                nc.scalar.copy(dst[:, 0:P // 2], src[:, 0:P // 2])
+                nc.vector.tensor_copy(dst[:, P // 2:P], src[:, P // 2:P])
             else:
                 nc.vector.tensor_copy(dst, src)
             return grouped
@@ -211,17 +212,28 @@ def tile_list_damped_grasp_scores_kernel(tc, tab_words, tab_scales, tab2_words, 
         def quantize_h(g, lo, hi):
             nc.vector.quantize_mx(out=h_codes[:, g, lo:hi].bitcast(FP8X4), scales=h_scale[:, g, lo:hi], in_=h_part(g, lo, hi))
 
+        def score_pass(y, c, g, lo, hi):
+            nc.tensor.matmul_mx(out=y, lhsT=w3_codes[:, g, c * P:(c + 1) * P].bitcast(FP8X4),
+                                lhsT_scale=w3_scale[:, g, :].bitcast(U8)[:, c * P:(c + 1) * P],
+                                rhs=h_codes[:, g, lo:hi].bitcast(FP8X4), rhs_scale=h_scale[:, g, lo:hi],
+                                start=(g == 0), stop=(g == GROUPS - 1))
+
         def scores(lo, hi):
-            y_bank = psum_by.tile([P, N // P, hi - lo], F32, name="y_bank", tag="bank")
             y_sb = ring.tile([P, N // P, hi - lo], F32, name="y_sb")
-            for c in range(N // P):
+            if hi < S:
+                y_bank = psum_by.tile([P, N // P, hi - lo], F32, name="y_bank", tag="bank")
+                for c in range(N // P):
+                    for g in range(GROUPS):
+                        score_pass(y_bank[:, c, :], c, g, lo, hi)
+                for c in range(N // P):
+                    nc.scalar.activation(y_sb[:, c, :], y_bank[:, c, :], ACT.Identity, bias=bias_sb[:, c:c + 1])
+            else:
+                y_last = [psum_by.tile([P, hi - lo], F32, name="y_last%d" % c, tag="bank") for c in range(N // P)]
                 for g in range(GROUPS):
-                    nc.tensor.matmul_mx(out=y_bank[:, c, :], lhsT=w3_codes[:, g, c * P:(c + 1) * P].bitcast(FP8X4),
-                                        lhsT_scale=w3_scale[:, g, :].bitcast(U8)[:, c * P:(c + 1) * P],
-                                        rhs=h_codes[:, g, lo:hi].bitcast(FP8X4), rhs_scale=h_scale[:, g, lo:hi],
-                                        start=(g == 0), stop=(g == GROUPS - 1))
-            for c in range(N // P):
-                nc.scalar.activation(y_sb[:, c, :], y_bank[:, c, :], ACT.Identity, bias=bias_sb[:, c:c + 1])
+                    for c in range(N // P):
+                        score_pass(y_last[c][:], c, g, lo, hi)
+                nc.vector.tensor_scalar(y_sb[:, 0, :], y_last[0][:], bias_sb[:, 0:1], None, ALU.add)
+                nc.scalar.activation(y_sb[:, 1, :], y_last[1][:], ACT.Identity, bias=bias_sb[:, 1:2])
             nc.sync.dma_start(out[:, lo:hi].rearrange("(c p) n -> p c n", p=P), y_sb[:])
 
         halves = ((0, S // 2), (S // 2, S))
@@ -238,18 +250,19 @@ def tile_list_damped_grasp_scores_kernel(tc, tab_words, tab_scales, tab2_words, 
             gather(v_codes[1], v_window[1][:].bitcast(U32), list1, lo, hi)
 
         release(0)
-        rounded = [round_w1(1, a) for a in range(K // PASS)]
+        rounded = [round_w1(1, 0)]
+        for n0 in range(0, 512, TOK):
+            damped(0, n0)
+        rounded.append(round_w1(1, 1))
         late_roots = held([P, 3 * span], F32, "late_roots", tag="w1_raw11")
         for i in range(5, 9):
             if i < 8:
                 root_of(i, late_roots[:, (i - 5) * span:(i - 4) * span])
             nc.scalar.activation(damp[:, 1, (i - 5) * span:(i - 4) * span], roots[i - 1], ACT.Square)
-        for n0 in range(0, 512, TOK):
-            damped(0, n0)
-        quantize_w1(1, 0, rounded[0])
         damped(0, 512)
         quantize_h(0, 0, 512)
         damped(0, 640)
+        quantize_w1(1, 0, rounded[0])
         quantize_w1(1, 1, rounded[1])
         h_late = held([P, 2 * TOK * PACK], BF16, "h_late", tag="grouped11")
         release(1)

@@ -53,12 +53,12 @@ def tile_list_damped_grasp_scores_kernel(tc, tab_words, tab_scales, tab2_words, 
         bias_sb = held([P, N // P], F32, "bias_sb")
         w1_raw = [[held([P, PACK, PASS], F32, "w1_raw%d%d" % (g, a)) for a in range(K // PASS)] for g in range(GROUPS)]
 
-        warm = held([P, 2], F32, "warm")
-        nc.vector.memset(u_scale_window[:], 0)
-        nc.vector.memset(w2_scale_raw[:], 0)
-        nc.vector.memset(warm[:, 0:1], 1.0)
-        nc.vector.memset(v_scale_window[:], 0)
-        nc.vector.memset(w3_scale[:], 0)
+        seed = held([P, 16], F32, "seed")
+        nc.gpsimd.memset(u_scale_window[:], 0)
+        nc.gpsimd.memset(w2_scale_raw[:], 0)
+        nc.vector.memset(seed[:, 0:1], 1.0)
+        nc.gpsimd.memset(v_scale_window[:], 0)
+        nc.gpsimd.memset(w3_scale[:], 0)
 
         def load_w1(g, a):
             rows = w1[a * PASS:(a + 1) * PASS, g * PASS:(g + 1) * PASS]
@@ -69,27 +69,28 @@ def tile_list_damped_grasp_scores_kernel(tc, tab_words, tab_scales, tab2_words, 
 
         nc.sync.dma_start(list2[:], offs2)
         for q in range(4):
-            nc.sync.dma_start(u_scale_window[32 * q:32 * q + 4, :], tab2_scales[0, 4 * q:4 * q + 4, :].bitcast(I32))
+            nc.sync.dma_start(u_scale_window[q:P:32, :], tab2_scales[0, q:16:4, :].bitcast(I32))
         nc.sync.dma_start(w2_raw[:], w2_words[0].bitcast(I32))
         nc.sync.dma_start(u_window[:], words_of(tab2_words[0]))
         for q in range(4):
-            nc.sync.dma_start(w2_scale_raw[32 * q:32 * q + 4, :], w2_scales[0, 4 * q:4 * q + 4, :].bitcast(I32))
-        nc.scalar.activation(warm[:, 1:2], warm[:, 0:1], ACT.Abs_reciprocal_sqrt)
-        for a in range(K // PASS):
-            load_w1(0, a)
-            if a == 1:
+            nc.sync.dma_start(w2_scale_raw[q:P:32, :], w2_scales[0, q:16:4, :].bitcast(I32))
+        nc.scalar.activation(seed[:, 1:2], seed[:, 0:1], ACT.Abs_reciprocal_sqrt)
+        nc.scalar.activation(seed[:, 8:9], seed[:, 1:2], ACT.Sign)
+        for i in range(K // PASS):
+            load_w1(0, i)
+            if i == 1:
                 nc.sync.dma_start(list1[:], offs)
-            for q in range(4):
-                nc.sync.dma_start(v_scale_window[32 * q + 4 * a:32 * q + 4 * a + 4, :],
-                                  tab_scales[a, 4 * q:4 * q + 4, :].bitcast(I32))
+            for r in (2 * i, 2 * i + 1):
+                for a in range(K // PASS):
+                    nc.sync.dma_start(v_scale_window[4 * a + r:P:32, :], tab_scales[a, r:16:4, :].bitcast(I32))
         for a in range(K // PASS):
             nc.sync.dma_start(v_window[a][:], words_of(tab_words[a]))
         load_w1(1, 0)
         load_w1(1, 1)
         nc.sync.dma_start(w3_codes[:], w3_words.rearrange("a p n t -> p a (n t)").bitcast(I32))
         for q in range(4):
-            nc.sync.dma_start(w3_scale[32 * q:32 * q + 4, :, :],
-                              w3_scales[:, 4 * q:4 * q + 4, :].rearrange("a r n -> r a n").bitcast(I32))
+            nc.sync.dma_start(w3_scale[q:P:32, :, :],
+                              w3_scales[:, q:16:4, :].rearrange("a r n -> r a n").bitcast(I32))
         with nc.allow_non_contiguous_dma(reason="one bias value to a partition"):
             nc.sync.dma_start(bias_sb[:], bias.rearrange("(c p) -> p c", p=P))
 
@@ -132,7 +133,7 @@ def tile_list_damped_grasp_scores_kernel(tc, tab_words, tab_scales, tab2_words, 
         def root_of(i, dst):
             g, c0 = spans[i]
             roots[i] = dst
-            nc.scalar.activation(dst, damp[:, g, c0:c0 + span], ACT.Abs_reciprocal_sqrt, bias=1.0)
+            nc.scalar.activation(dst, damp[:, g, c0:c0 + span], ACT.Abs_reciprocal_sqrt, bias=seed[:, 8:9])
 
         for n0 in range(0, S, TOK):
             square_b(0, n0)
@@ -240,7 +241,6 @@ def tile_list_damped_grasp_scores_kernel(tc, tab_words, tab_scales, tab2_words, 
         rounded = [round_w1(0, a) for a in range(K // PASS)]
         for a in range(K // PASS):
             quantize_w1(0, a, rounded[a])
-        early_damp = held([P, len(ON_VECTOR) * span], F32, "early_damp", tag="grouped01")
         early_damp = held([P, len(ON_VECTOR) * span], F32, "early_damp", tag="grouped01")
         for i in ON_VECTOR:
             square_root_on_vector(i)

@@ -33,6 +33,7 @@ def tile_list_damped_grasp_scores_kernel(tc, tab_words, tab_scales, tab2_words, 
     nc = tc.nc
     with ExitStack() as ctx:
         keep = ctx.enter_context(tc.tile_pool(name="keep", bufs=1))
+        early = ctx.enter_context(tc.tile_pool(name="early", bufs=1))
         ring = ctx.enter_context(tc.tile_pool(name="ring", bufs=4))
         psum_ab = ctx.enter_context(tc.psum_pool(name="psum_ab", bufs=BANKS))
         psum_by = ctx.enter_context(tc.psum_pool(name="psum_by", bufs=4))
@@ -47,7 +48,7 @@ def tile_list_damped_grasp_scores_kernel(tc, tab_words, tab_scales, tab2_words, 
         u_window = held([P, T2], I32, "u_window")
         u_scale_window = held([P, T2 // 4], I32, "u_scale_window")
         w2_raw = held([P, H // 2], I32, "w2_raw")
-        w2_scale_raw = held([P, H // 4], I32, "w2_scale_raw")
+        w2_scale_raw = early.tile([P, H // 4], I32, name="w2_scale_raw", align_bytes=64, offset=0)
         w3_codes = held([P, GROUPS, N], I32, "w3_codes")
         w3_scale = held([P, GROUPS, N // 4], I32, "w3_scale")
         bias_sb = held([P, N // P], F32, "bias_sb")
@@ -99,17 +100,22 @@ def tile_list_damped_grasp_scores_kernel(tc, tab_words, tab_scales, tab2_words, 
 
         w2_codes = held([P, 2 * H], U8, "w2_codes")
         w2_scale = held([P, H], U8, "w2_scale")
-        u_scale = held([P, S], U8, "u_scale")
-        gather(u_scale, u_scale_window[:].bitcast(U8), list2, 0, S)
+        u_scale_first = held([P, S // 2], U8, "u_scale_first")
+        gather(u_scale_first, u_scale_window[:].bitcast(U8), list2, 0, S // 2)
         nc.vector.tensor_copy(w2_codes[:].bitcast(U16).rearrange("p (g t m) -> p g t m", g=GROUPS, t=PACK),
                               w2_raw[:].bitcast(U16).rearrange("p (g m t) -> p g t m", g=GROUPS, t=PACK))
         u_first = held([P, FIRST], U32, "u_first")
         gather(u_first, u_window[:].bitcast(U32), list2, 0, FIRST)
-        nc.vector.tensor_copy(w2_scale[:].rearrange("p (g t m) -> p g t m", g=GROUPS, t=PACK),
-                              w2_scale_raw[:].bitcast(U8).rearrange("p (g m t) -> p g t m", g=GROUPS, t=PACK))
-        u_rest = held([P, S], U32, "u_rest", tag="w2_scale_raw")
-        for lo, hi in ((FIRST, 2 * FIRST), (2 * FIRST, S)):
-            gather(u_rest, u_window[:].bitcast(U32), list2, lo, hi)
+        for g in range(GROUPS):
+            cols = slice(g * PASS, (g + 1) * PASS)
+            nc.vector.tensor_copy(w2_scale[:, cols].rearrange("p (t m) -> p t m", t=PACK),
+                                  w2_scale_raw[:].bitcast(U8)[:, cols].rearrange("p (m t) -> p t m", t=PACK))
+        u_scale_rest = early.tile([P, S // 2], U8, name="u_scale_rest", align_bytes=64, offset=0)
+        u_rest = early.tile([P, S], U32, name="u_rest", align_bytes=64, offset=S // 2)
+        gather(u_rest, u_window[:].bitcast(U32), list2, FIRST, 2 * FIRST)
+        nc.vector.tensor_copy(u_scale_rest[:], u_scale_window[:].bitcast(U8).indirect(list2[:, S // 32:S // 16]))
+        gather(u_rest, u_window[:].bitcast(U32), list2, 2 * FIRST, 3 * FIRST)
+        gather(u_rest, u_window[:].bitcast(U32), list2, 3 * FIRST, S)
 
         damp = held([P, GROUPS, S * PACK], F32, "damp")
 
@@ -120,7 +126,7 @@ def tile_list_damped_grasp_scores_kernel(tc, tab_words, tab_scales, tab2_words, 
                 m0 = g * PASS + t * P
                 nc.tensor.matmul_mx(out=b_bank[:, t, :], lhsT=w2_codes[:, 2 * m0:2 * (m0 + P)].bitcast(FP4X4),
                                     lhsT_scale=w2_scale[:, m0:m0 + P], rhs=(u_first if n0 < FIRST else u_rest)[:, cols].bitcast(FP8X4),
-                                    rhs_scale=u_scale[:, cols], start=True, stop=True)
+                                    rhs_scale=u_scale_first[:, cols] if n0 < S // 2 else u_scale_rest[:, n0 - S // 2:n0 - S // 2 + TOK], start=True, stop=True)
             nc.scalar.activation(damp[:, g, n0 * PACK:(n0 + TOK) * PACK].rearrange("p (n t) -> p n t", t=PACK),
                                  b_bank[:].rearrange("p t n -> p n t"), ACT.Square)
 
@@ -139,10 +145,11 @@ def tile_list_damped_grasp_scores_kernel(tc, tab_words, tab_scales, tab2_words, 
             square_b(0, n0)
         for i in range(4):
             root_of(i, early_roots[:, i * span:(i + 1) * span])
-        for i in range(len(ON_VECTOR), 4):
-            nc.scalar.activation(damp[:, 0, i * span:(i + 1) * span], roots[i], ACT.Square)
+        nc.scalar.activation(damp[:, 0, span:2 * span], roots[1], ACT.Square)
         for n0 in range(0, S, TOK):
             square_b(1, n0)
+        for i in (2, 3):
+            nc.scalar.activation(damp[:, 0, i * span:(i + 1) * span], roots[i], ACT.Square)
         root_of(4, early_roots[:, 4 * span:5 * span])
 
         def square_root_on_vector(i):
@@ -175,26 +182,20 @@ def tile_list_damped_grasp_scores_kernel(tc, tab_words, tab_scales, tab2_words, 
         h_codes = held([P, GROUPS, S], U32, "h_codes")
         h_scale = held([P, GROUPS, S], U8, "h_scale")
 
-        def project(g, n0):
-            cols = slice(n0, n0 + TOK)
-            a_bank = psum_ab.tile([P, PACK, TOK], F32, name="a_bank", tag="bank")
-            for t in range(PACK):
-                m_cols = slice(t * P, (t + 1) * P)
-                for a in range(K // PASS):
-                    nc.tensor.matmul_mx(out=a_bank[:, t, :], lhsT=w1_codes[:, g, a, m_cols].bitcast(FP8X4),
-                                        lhsT_scale=w1_scale[:, g, a, m_cols],
-                                        rhs=v_codes[a][:, cols].bitcast(FP8X4), rhs_scale=v_scale[4 * a:P, cols],
-                                        start=(a == 0), stop=(a == K // PASS - 1))
-            a_banks[g, n0] = a_bank
-
         h_bf = held([P, GROUPS, S * PACK], BF16, "h_bf")
         a_banks = {}
         waiting = []
 
-        def release(g):
-            waiting.extend((g, n0) for n0 in range(0, S, TOK))
-            while waiting and len(a_banks) < BANKS:
-                project(*waiting.pop(0))
+        def project(g, n0, a):
+            cols = slice(n0, n0 + TOK)
+            if a == 0:
+                a_banks[g, n0] = psum_ab.tile([P, PACK, TOK], F32, name="a_bank", tag="bank")
+            for t in range(PACK):
+                m_cols = slice(t * P, (t + 1) * P)
+                nc.tensor.matmul_mx(out=a_banks[g, n0][:, t, :], lhsT=w1_codes[:, g, a, m_cols].bitcast(FP8X4),
+                                    lhsT_scale=w1_scale[:, g, a, m_cols],
+                                    rhs=v_codes[a][:, cols].bitcast(FP8X4), rhs_scale=v_scale[4 * a:P, cols],
+                                    start=(a == 0 and t == 0), stop=(a == 1 and t == PACK - 1))
 
         def h_part(g, lo, hi):
             if g == 0 and lo >= LATE:
@@ -208,31 +209,39 @@ def tile_list_damped_grasp_scores_kernel(tc, tab_words, tab_scales, tab2_words, 
                                     a_banks.pop((g, n0))[:].rearrange("p t n -> p n t"),
                                     factor.rearrange("p (n t) -> p n t", t=PACK), ALU.mult)
             if waiting:
-                project(*waiting.pop(0))
+                ahead = waiting.pop(0)
+                project(*ahead, 0)
+                project(*ahead, 1)
 
         def quantize_h(g, lo, hi):
             nc.vector.quantize_mx(out=h_codes[:, g, lo:hi].bitcast(FP8X4), scales=h_scale[:, g, lo:hi], in_=h_part(g, lo, hi))
 
-        def score_pass(y, c, g, lo, hi):
+        def score_pass(y, c, g, lo, hi, start, stop):
             nc.tensor.matmul_mx(out=y, lhsT=w3_codes[:, g, c * P:(c + 1) * P].bitcast(FP8X4),
                                 lhsT_scale=w3_scale[:, g, :].bitcast(U8)[:, c * P:(c + 1) * P],
                                 rhs=h_codes[:, g, lo:hi].bitcast(FP8X4), rhs_scale=h_scale[:, g, lo:hi],
-                                start=(g == 0), stop=(g == GROUPS - 1))
+                                start=start, stop=stop)
+
+        y_banks = {}
+
+        def open_scores(lo, hi):
+            y_banks[lo] = psum_by.tile([P, N // P, hi - lo], F32, name="y_bank", tag="bank")
+            for c in range(N // P):
+                score_pass(y_banks[lo][:, c, :], c, 0, lo, hi, c == 0, False)
 
         def scores(lo, hi):
             y_sb = ring.tile([P, N // P, hi - lo], F32, name="y_sb")
             if hi < S:
-                y_bank = psum_by.tile([P, N // P, hi - lo], F32, name="y_bank", tag="bank")
+                y_bank = y_banks.pop(lo)
                 for c in range(N // P):
-                    for g in range(GROUPS):
-                        score_pass(y_bank[:, c, :], c, g, lo, hi)
+                    score_pass(y_bank[:, c, :], c, 1, lo, hi, False, c == N // P - 1)
                 for c in range(N // P):
                     nc.scalar.activation(y_sb[:, c, :], y_bank[:, c, :], ACT.Identity, bias=bias_sb[:, c:c + 1])
             else:
                 y_last = [psum_by.tile([P, hi - lo], F32, name="y_last%d" % c, tag="bank") for c in range(N // P)]
                 for g in range(GROUPS):
                     for c in range(N // P):
-                        score_pass(y_last[c][:], c, g, lo, hi)
+                        score_pass(y_last[c][:], c, g, lo, hi, g == 0, g == GROUPS - 1)
                 nc.vector.tensor_scalar(y_sb[:, 0, :], y_last[0][:], bias_sb[:, 0:1], None, ALU.add)
                 nc.scalar.activation(y_sb[:, 1, :], y_last[1][:], ACT.Identity, bias=bias_sb[:, 1:2])
             nc.sync.dma_start(out[:, lo:hi].rearrange("(c p) n -> p c n", p=P), y_sb[:])
@@ -246,10 +255,14 @@ def tile_list_damped_grasp_scores_kernel(tc, tab_words, tab_scales, tab2_words, 
             square_root_on_vector(i)
         gather(v_scale, v_scale_window[:].bitcast(U8), list1, 0, S)
         gather(v_codes[0], v_window[0][:].bitcast(U32), list1, 0, S)
+        for n0 in range(0, BANKS * TOK, TOK):
+            project(0, n0, 0)
         for lo, hi in halves:
             gather(v_codes[1], v_window[1][:].bitcast(U32), list1, lo, hi)
 
-        release(0)
+        for n0 in range(0, BANKS * TOK, TOK):
+            project(0, n0, 1)
+        waiting.extend((0, n0) for n0 in range(BANKS * TOK, S, TOK))
         rounded = [round_w1(1, 0)]
         for n0 in range(0, 512, TOK):
             damped(0, n0)
@@ -261,16 +274,24 @@ def tile_list_damped_grasp_scores_kernel(tc, tab_words, tab_scales, tab2_words, 
             nc.scalar.activation(damp[:, 1, (i - 5) * span:(i - 4) * span], roots[i - 1], ACT.Square)
         damped(0, 512)
         quantize_h(0, 0, 512)
+        open_scores(0, 256)
+        open_scores(256, 512)
         damped(0, 640)
         quantize_w1(1, 0, rounded[0])
+        for n0 in (0, TOK):
+            project(1, n0, 0)
         quantize_w1(1, 1, rounded[1])
         h_late = held([P, 2 * TOK * PACK], BF16, "h_late", tag="grouped11")
-        release(1)
+        for n0 in (0, TOK):
+            project(1, n0, 1)
+        waiting.extend((1, n0) for n0 in range(2 * TOK, S, TOK))
         damped(0, 768)
         quantize_h(0, 512, 768)
+        open_scores(512, 768)
         damped(0, 896)
         damped(1, 0)
         quantize_h(0, 768, 1024)
+        open_scores(768, 896)
         chunks = ((0, 256), (256, 512), (512, 768), (768, 896), (896, 1024))
         done = 128
         for lo, hi in chunks:

@@ -22,8 +22,9 @@ PASS = P * PACK
 TOK = 128
 GROUPS = H // PASS
 BLOCKS = S // TOK
-BANKS = 4
-LATE = 768
+BANKS = 3
+LATE = 896
+SPLIT = 64
 FIRST = 256
 ON_VECTOR = (0,)
 
@@ -52,7 +53,8 @@ def tile_list_damped_grasp_scores_kernel(tc, tab_words, tab_scales, tab2_words, 
         w3_codes = held([P, GROUPS, N], I32, "w3_codes")
         w3_scale = held([P, GROUPS, N // 4], I32, "w3_scale")
         bias_sb = held([P, N // P], F32, "bias_sb")
-        w1_raw = [[held([P, PACK, PASS], F32, "w1_raw%d%d" % (g, a)) for a in range(K // PASS)] for g in range(GROUPS)]
+        w1_raw = [[held([P, PACK, PASS], F32, "w1_raw%d%d" % (g, a)) for a in range(K // PASS - g)] for g in range(GROUPS)]
+        last_raw = [held([P, PACK, PACK * SPLIT], F32, "last_raw0"), held([P, PACK, PASS - PACK * SPLIT], F32, "last_raw1")]
 
         seed = held([P, 16], F32, "seed")
         nc.gpsimd.memset(u_scale_window[:], 0)
@@ -87,7 +89,9 @@ def tile_list_damped_grasp_scores_kernel(tc, tab_words, tab_scales, tab2_words, 
         for a in range(K // PASS):
             nc.sync.dma_start(v_window[a][:], words_of(tab_words[a]))
         load_w1(1, 0)
-        load_w1(1, 1)
+        last_rows = w1[PASS:K, PASS:H].rearrange("(p j) c -> p j c", j=PACK)
+        nc.sync.dma_start(last_raw[0][:], last_rows[:, :, 0:PACK * SPLIT])
+        nc.sync.dma_start(last_raw[1][:], last_rows[:, :, PACK * SPLIT:PASS])
         nc.sync.dma_start(w3_codes[:], w3_words.rearrange("a p n t -> p a (n t)").bitcast(I32))
         for q in range(4):
             nc.sync.dma_start(w3_scale[q:P:32, :, :],
@@ -166,9 +170,6 @@ def tile_list_damped_grasp_scores_kernel(tc, tab_words, tab_scales, tab2_words, 
             if (g, a) in ((1, 0),):
                 for m0 in range(0, P, 32):
                     nc.gpsimd.tensor_scalar(dst[:, m0:m0 + 32], src[:, m0:m0 + 32], 1.0, 0.0, ALU.mult, ALU.add)
-            elif (g, a) in ((1, 1),):
-                nc.scalar.copy(dst[:, 0:P // 2], src[:, 0:P // 2])
-                nc.vector.tensor_copy(dst[:, P // 2:P], src[:, P // 2:P])
             else:
                 nc.vector.tensor_copy(dst, src)
             return grouped
@@ -179,7 +180,7 @@ def tile_list_damped_grasp_scores_kernel(tc, tab_words, tab_scales, tab2_words, 
 
         v_codes = [held([P, S], U32, "v_codes%d" % a) for a in range(K // PASS)]
         v_scale = held([P, S], U8, "v_scale")
-        h_codes = held([P, GROUPS, S], U32, "h_codes")
+        h_codes = {1: held([P, S], U32, "h_codes1")}
         h_scale = held([P, GROUPS, S], U8, "h_scale")
 
         h_bf = held([P, GROUPS, S * PACK], BF16, "h_bf")
@@ -214,12 +215,12 @@ def tile_list_damped_grasp_scores_kernel(tc, tab_words, tab_scales, tab2_words, 
                 project(*ahead, 1)
 
         def quantize_h(g, lo, hi):
-            nc.vector.quantize_mx(out=h_codes[:, g, lo:hi].bitcast(FP8X4), scales=h_scale[:, g, lo:hi], in_=h_part(g, lo, hi))
+            nc.vector.quantize_mx(out=h_codes[g][:, lo:hi].bitcast(FP8X4), scales=h_scale[:, g, lo:hi], in_=h_part(g, lo, hi))
 
         def score_pass(y, c, g, lo, hi, start, stop):
             nc.tensor.matmul_mx(out=y, lhsT=w3_codes[:, g, c * P:(c + 1) * P].bitcast(FP8X4),
                                 lhsT_scale=w3_scale[:, g, :].bitcast(U8)[:, c * P:(c + 1) * P],
-                                rhs=h_codes[:, g, lo:hi].bitcast(FP8X4), rhs_scale=h_scale[:, g, lo:hi],
+                                rhs=h_codes[g][:, lo:hi].bitcast(FP8X4), rhs_scale=h_scale[:, g, lo:hi],
                                 start=start, stop=stop)
 
         y_banks = {}
@@ -264,34 +265,36 @@ def tile_list_damped_grasp_scores_kernel(tc, tab_words, tab_scales, tab2_words, 
             project(0, n0, 1)
         waiting.extend((0, n0) for n0 in range(BANKS * TOK, S, TOK))
         rounded = [round_w1(1, 0)]
-        for n0 in range(0, 512, TOK):
+        for n0 in range(0, LATE, TOK):
             damped(0, n0)
-        rounded.append(round_w1(1, 1))
-        late_roots = held([P, 3 * span], F32, "late_roots", tag="w1_raw11")
+        rounded.append(held([P, PACK, P, PACK], BF16, "grouped11"))
+        last_dst = rounded[1][:].rearrange("p t m j -> p m t j")
+        nc.scalar.copy(last_dst[:, 0:SPLIT], last_raw[0][:].rearrange("p j (m t) -> p m t j", t=PACK))
+        late_roots = held([P, 3 * span], F32, "late_roots", tag="last_raw0")
         for i in range(5, 9):
             if i < 8:
                 root_of(i, late_roots[:, (i - 5) * span:(i - 4) * span])
             nc.scalar.activation(damp[:, 1, (i - 5) * span:(i - 4) * span], roots[i - 1], ACT.Square)
-        damped(0, 512)
+        quantize_w1(1, 0, rounded[0])
+        for n0 in range(0, (BANKS - 1) * TOK, TOK):
+            project(1, n0, 0)
+        nc.vector.tensor_copy(last_dst[:, SPLIT:P], last_raw[1][:].rearrange("p j (m t) -> p m t j", t=PACK))
+        h_codes[0] = held([P, S], U32, "h_codes0", tag="grouped10")
         quantize_h(0, 0, 512)
         open_scores(0, 256)
         open_scores(256, 512)
-        damped(0, 640)
-        quantize_w1(1, 0, rounded[0])
-        for n0 in (0, TOK):
-            project(1, n0, 0)
         quantize_w1(1, 1, rounded[1])
-        h_late = held([P, 2 * TOK * PACK], BF16, "h_late", tag="grouped11")
-        for n0 in (0, TOK):
+        h_late = held([P, TOK * PACK], BF16, "h_late", tag="grouped11")
+        for n0 in range(0, (BANKS - 1) * TOK, TOK):
             project(1, n0, 1)
-        waiting.extend((1, n0) for n0 in range(2 * TOK, S, TOK))
-        damped(0, 768)
+        waiting.extend((1, n0) for n0 in range((BANKS - 1) * TOK, S, TOK))
+        damped(0, 896)
         quantize_h(0, 512, 768)
         open_scores(512, 768)
-        damped(0, 896)
-        damped(1, 0)
-        quantize_h(0, 768, 1024)
+        quantize_h(0, 768, 896)
         open_scores(768, 896)
+        damped(1, 0)
+        quantize_h(0, 896, 1024)
         chunks = ((0, 256), (256, 512), (512, 768), (768, 896), (896, 1024))
         done = 128
         for lo, hi in chunks:

@@ -24,9 +24,7 @@ GROUPS = H // PASS
 BLOCKS = S // TOK
 BANKS = 3
 LATE = 896
-SPLIT = 64
 FIRST = 256
-ON_VECTOR = (0,)
 
 
 def tile_list_damped_grasp_scores_kernel(tc, tab_words, tab_scales, tab2_words, tab2_scales, offs, offs2, w1,
@@ -44,28 +42,26 @@ def tile_list_damped_grasp_scores_kernel(tc, tab_words, tab_scales, tab2_words, 
 
         list1 = keep.tile([P, S // 16], U16, name="list1")
         list2 = keep.tile([P, S // 16], U16, name="list2")
-        v_window = [held([P, T], I32, "v_window%d" % a) for a in range(K // PASS)]
-        v_scale_window = held([P, T // 4], I32, "v_scale_window")
+        v_window = [held([P, T], I32, "v_window0")]
+        v_scale_window = held([P, T // 4], I32, "v_scale_window", tag="v_window1")
+        v_scale = held([P, S // 4], I32, "v_scale")
         u_window = held([P, T2], I32, "u_window")
         u_scale_window = held([P, T2 // 4], I32, "u_scale_window")
         w2_raw = held([P, H // 2], I32, "w2_raw")
         w2_scale_raw = early.tile([P, H // 4], I32, name="w2_scale_raw", align_bytes=64, offset=0)
-        w3_codes = held([P, GROUPS, N], I32, "w3_codes")
-        w3_scale = held([P, GROUPS, N // 4], I32, "w3_scale")
-        bias_sb = held([P, N // P], F32, "bias_sb")
-        w1_raw = [[held([P, PACK, PASS], F32, "w1_raw%d%d" % (g, a)) for a in range(K // PASS - g)] for g in range(GROUPS)]
-        last_raw = [held([P, PACK, PACK * SPLIT], F32, "last_raw0"), held([P, PACK, PASS - PACK * SPLIT], F32, "last_raw1")]
+        w1_raw = {}
 
         seed = held([P, 16], F32, "seed")
         nc.gpsimd.memset(u_scale_window[:], 0)
         nc.gpsimd.memset(w2_scale_raw[:], 0)
         nc.vector.memset(seed[:, 0:1], 1.0)
         nc.gpsimd.memset(v_scale_window[:], 0)
-        nc.gpsimd.memset(w3_scale[:], 0)
+        nc.gpsimd.memset(v_scale[:], 0)
 
         def load_w1(g, a):
             rows = w1[a * PASS:(a + 1) * PASS, g * PASS:(g + 1) * PASS]
-            nc.sync.dma_start(w1_raw[g][a][:], rows.rearrange("(p j) c -> p j c", j=PACK))
+            w1_raw[g, a] = held([P, PACK, PASS], F32, "w1_raw%d%d" % (g, a), tag="w1_raw%d" % a)
+            nc.sync.dma_start(w1_raw[g, a][:], rows.rearrange("(p j) c -> p j c", j=PACK))
 
         def words_of(packed):
             return packed.rearrange("p n t -> p (n t)").bitcast(I32)
@@ -79,25 +75,11 @@ def tile_list_damped_grasp_scores_kernel(tc, tab_words, tab_scales, tab2_words, 
             nc.sync.dma_start(w2_scale_raw[q:P:32, :], w2_scales[0, q:16:4, :].bitcast(I32))
         nc.scalar.activation(seed[:, 1:2], seed[:, 0:1], ACT.Abs_reciprocal_sqrt)
         nc.scalar.activation(seed[:, 8:9], seed[:, 1:2], ACT.Sign)
-        for i in range(K // PASS):
-            load_w1(0, i)
-            if i == 1:
-                nc.sync.dma_start(list1[:], offs)
-            for r in (2 * i, 2 * i + 1):
-                for a in range(K // PASS):
-                    nc.sync.dma_start(v_scale_window[4 * a + r:P:32, :], tab_scales[a, r:16:4, :].bitcast(I32))
+        nc.sync.dma_start(v_scale_window[0:P:4, :], tab_scales.rearrange("a q n -> (a q) n").bitcast(I32))
+        nc.sync.dma_start(list1[:], offs)
         for a in range(K // PASS):
-            nc.sync.dma_start(v_window[a][:], words_of(tab_words[a]))
-        load_w1(1, 0)
-        last_rows = w1[PASS:K, PASS:H].rearrange("(p j) c -> p j c", j=PACK)
-        nc.sync.dma_start(last_raw[0][:], last_rows[:, :, 0:PACK * SPLIT])
-        nc.sync.dma_start(last_raw[1][:], last_rows[:, :, PACK * SPLIT:PASS])
-        nc.sync.dma_start(w3_codes[:], w3_words.rearrange("a p n t -> p a (n t)").bitcast(I32))
-        for q in range(4):
-            nc.sync.dma_start(w3_scale[q:P:32, :, :],
-                              w3_scales[:, q:16:4, :].rearrange("a r n -> r a n").bitcast(I32))
-        with nc.allow_non_contiguous_dma(reason="one bias value to a partition"):
-            nc.sync.dma_start(bias_sb[:], bias.rearrange("(c p) -> p c", p=P))
+            load_w1(0, a)
+        nc.sync.dma_start(v_window[0][:], words_of(tab_words[0]))
 
         def gather(dst, window, offsets, lo, hi):
             nc.vector.tensor_copy(dst[:, lo:hi], window.indirect(offsets[:, lo // 16:hi // 16]))
@@ -121,6 +103,19 @@ def tile_list_damped_grasp_scores_kernel(tc, tab_words, tab_scales, tab2_words, 
         gather(u_rest, u_window[:].bitcast(U32), list2, 2 * FIRST, 3 * FIRST)
         gather(u_rest, u_window[:].bitcast(U32), list2, 3 * FIRST, S)
 
+        v_scale_picked = held([P, S], U8, "v_scale_picked")
+        gather(v_scale_picked, v_scale_window[:].bitcast(U8), list1, 0, S)
+
+        def place_scale_rows(a):
+            for r in range(4):
+                first = 64 * a + 4 * r
+                nc.sync.dma_start(v_scale[4 * a + r:P:32, :], v_scale_picked[:].bitcast(I32)[first:first + 49:16, :])
+
+        place_scale_rows(0)
+        v_window.append(held([P, T], I32, "v_window1"))
+        nc.sync.dma_start(v_window[1][:], words_of(tab_words[1]))
+        place_scale_rows(1)
+
         damp = held([P, GROUPS, S * PACK], F32, "damp")
 
         def square_b(g, n0):
@@ -136,36 +131,34 @@ def tile_list_damped_grasp_scores_kernel(tc, tab_words, tab_scales, tab2_words, 
 
         span = 2 * TOK * PACK
         spans = [(g, i * span) for g in range(GROUPS) for i in range(BLOCKS // 2)]
-        roots = {}
+        early_roots = held([P, 5, span], F32, "early_roots")
+        roots = [early_roots[:, i, :] for i in range(5)]
 
-        early_roots = held([P, 5 * span], F32, "early_roots")
-
-        def root_of(i, dst):
+        def root_of(i):
             g, c0 = spans[i]
-            roots[i] = dst
-            nc.scalar.activation(dst, damp[:, g, c0:c0 + span], ACT.Abs_reciprocal_sqrt, bias=seed[:, 8:9])
+            nc.scalar.activation(roots[i], damp[:, g, c0:c0 + span], ACT.Abs_reciprocal_sqrt, bias=seed[:, 8:9])
+
+        def square_root(i, lo=0, hi=span):
+            g, c0 = spans[i]
+            nc.scalar.activation(damp[:, g, c0 + lo:c0 + hi], roots[i][:, lo:hi], ACT.Square)
 
         for n0 in range(0, S, TOK):
             square_b(0, n0)
         for i in range(4):
-            root_of(i, early_roots[:, i * span:(i + 1) * span])
-        nc.scalar.activation(damp[:, 0, span:2 * span], roots[1], ACT.Square)
+            root_of(i)
+        square_root(1)
         for n0 in range(0, S, TOK):
             square_b(1, n0)
         for i in (2, 3):
-            nc.scalar.activation(damp[:, 0, i * span:(i + 1) * span], roots[i], ACT.Square)
-        root_of(4, early_roots[:, 4 * span:5 * span])
-
-        def square_root_on_vector(i):
-            g, c0 = spans[i]
-            nc.vector.tensor_tensor(early_damp[:, c0:c0 + span], roots[i], roots[i], ALU.mult)
+            square_root(i)
+        root_of(4)
 
         w1_codes = held([P, GROUPS, K // PASS, PASS], U32, "w1_codes")
         w1_scale = held([P, GROUPS, K // PASS, PASS], U8, "w1_scale")
 
         def round_w1(g, a):
             grouped = held([P, PACK, P, PACK], BF16, "grouped%d%d" % (g, a))
-            src = w1_raw[g][a][:].rearrange("p j (m t) -> p m t j", t=PACK)
+            src = w1_raw[g, a][:].rearrange("p j (m t) -> p m t j", t=PACK)
             dst = grouped[:].rearrange("p t m j -> p m t j")
             if (g, a) in ((1, 0),):
                 for m0 in range(0, P, 32):
@@ -179,7 +172,6 @@ def tile_list_damped_grasp_scores_kernel(tc, tab_words, tab_scales, tab2_words, 
                                   in_=grouped[:].rearrange("p t m j -> p (t m j)"))
 
         v_codes = [held([P, S], U32, "v_codes%d" % a) for a in range(K // PASS)]
-        v_scale = held([P, S], U8, "v_scale")
         h_codes = {1: held([P, S], U32, "h_codes1")}
         h_scale = held([P, GROUPS, S], U8, "h_scale")
 
@@ -195,7 +187,7 @@ def tile_list_damped_grasp_scores_kernel(tc, tab_words, tab_scales, tab2_words, 
                 m_cols = slice(t * P, (t + 1) * P)
                 nc.tensor.matmul_mx(out=a_banks[g, n0][:, t, :], lhsT=w1_codes[:, g, a, m_cols].bitcast(FP8X4),
                                     lhsT_scale=w1_scale[:, g, a, m_cols],
-                                    rhs=v_codes[a][:, cols].bitcast(FP8X4), rhs_scale=v_scale[4 * a:P, cols],
+                                    rhs=v_codes[a][:, cols].bitcast(FP8X4), rhs_scale=v_scale[:].bitcast(U8)[4 * a:P, cols],
                                     start=(a == 0 and t == 0), stop=(a == 1 and t == PACK - 1))
 
         def h_part(g, lo, hi):
@@ -205,7 +197,7 @@ def tile_list_damped_grasp_scores_kernel(tc, tab_words, tab_scales, tab2_words, 
 
         def damped(g, n0):
             cols = slice(n0 * PACK, (n0 + TOK) * PACK)
-            factor = early_damp[:, cols] if g == 0 and cols.stop <= len(ON_VECTOR) * span else damp[:, g, cols]
+            factor = early_damp[:, cols] if g == 0 and cols.stop <= span else damp[:, g, cols]
             nc.vector.tensor_tensor(h_part(g, n0, n0 + TOK).rearrange("p (n t) -> p n t", t=PACK),
                                     a_banks.pop((g, n0))[:].rearrange("p t n -> p n t"),
                                     factor.rearrange("p (n t) -> p n t", t=PACK), ALU.mult)
@@ -251,11 +243,24 @@ def tile_list_damped_grasp_scores_kernel(tc, tab_words, tab_scales, tab2_words, 
         rounded = [round_w1(0, a) for a in range(K // PASS)]
         for a in range(K // PASS):
             quantize_w1(0, a, rounded[a])
-        early_damp = held([P, len(ON_VECTOR) * span], F32, "early_damp", tag="grouped01")
-        for i in ON_VECTOR:
-            square_root_on_vector(i)
-        gather(v_scale, v_scale_window[:].bitcast(U8), list1, 0, S)
+        load_w1(1, 0)
+        last_rows = w1[PASS:K, PASS:H].rearrange("(p j) c -> p j c", j=PACK)
+        last_raw = [held([P, PACK, PASS // 2], F32, "last_raw%d" % i, tag=tag) for i, tag in enumerate(("w1_raw1", "grouped00"))]
+        for i in range(2):
+            nc.sync.dma_start(last_raw[i][:], last_rows[:, :, i * PASS // 2:(i + 1) * PASS // 2])
+        early_damp = held([P, span], F32, "early_damp", tag="grouped01")
+        nc.vector.tensor_tensor(early_damp[:], roots[0], roots[0], ALU.mult)
         gather(v_codes[0], v_window[0][:].bitcast(U32), list1, 0, S)
+        w3_codes = held([P, GROUPS, N], I32, "w3_codes", tag="v_scale_picked")
+        nc.sync.dma_start(w3_codes[:], w3_words.rearrange("a p n t -> p a (n t)").bitcast(I32))
+        w3_scale = held([P, GROUPS, N // 4], I32, "w3_scale", tag="v_window0")
+        nc.vector.memset(w3_scale[:], 0)
+        for q in range(4):
+            nc.sync.dma_start(w3_scale[q:P:32, :, :],
+                              w3_scales[:, q:16:4, :].rearrange("a r n -> r a n").bitcast(I32))
+        bias_sb = held([P, N // P], F32, "bias_sb", tag="u_first")
+        with nc.allow_non_contiguous_dma(reason="one bias value to a partition"):
+            nc.sync.dma_start(bias_sb[:], bias.rearrange("(c p) -> p c", p=P))
         for n0 in range(0, BANKS * TOK, TOK):
             project(0, n0, 0)
         for lo, hi in halves:
@@ -269,16 +274,18 @@ def tile_list_damped_grasp_scores_kernel(tc, tab_words, tab_scales, tab2_words, 
             damped(0, n0)
         rounded.append(held([P, PACK, P, PACK], BF16, "grouped11"))
         last_dst = rounded[1][:].rearrange("p t m j -> p m t j")
-        nc.scalar.copy(last_dst[:, 0:SPLIT], last_raw[0][:].rearrange("p j (m t) -> p m t j", t=PACK))
-        late_roots = held([P, 3 * span], F32, "late_roots", tag="last_raw0")
-        for i in range(5, 9):
-            if i < 8:
-                root_of(i, late_roots[:, (i - 5) * span:(i - 4) * span])
-            nc.scalar.activation(damp[:, 1, (i - 5) * span:(i - 4) * span], roots[i - 1], ACT.Square)
+        nc.scalar.copy(last_dst[:, 0:P // 2], last_raw[0][:].rearrange("p j (m t) -> p m t j", t=PACK))
+        late_roots = held([P, 3, span], F32, "late_roots", tag="w1_raw1")
+        roots.extend(late_roots[:, i, :] for i in range(3))
+        for i in range(5, 8):
+            root_of(i)
+            square_root(i - 1)
+        square_root(7, 0, span // 2)
+        square_root(7, span // 2, span)
         quantize_w1(1, 0, rounded[0])
         for n0 in range(0, (BANKS - 1) * TOK, TOK):
             project(1, n0, 0)
-        nc.vector.tensor_copy(last_dst[:, SPLIT:P], last_raw[1][:].rearrange("p j (m t) -> p m t j", t=PACK))
+        nc.vector.tensor_copy(last_dst[:, P // 2:P], last_raw[1][:].rearrange("p j (m t) -> p m t j", t=PACK))
         h_codes[0] = held([P, S], U32, "h_codes0", tag="grouped10")
         quantize_h(0, 0, 512)
         open_scores(0, 256)

@@ -25,6 +25,7 @@ BLOCKS = S // TOK
 BANKS = 3
 LATE = 896
 FIRST = 256
+EARLY = TOK * PACK
 
 
 def tile_list_damped_grasp_scores_kernel(tc, tab_words, tab_scales, tab2_words, tab2_scales, offs, offs2, w1,
@@ -131,8 +132,8 @@ def tile_list_damped_grasp_scores_kernel(tc, tab_words, tab_scales, tab2_words, 
 
         span = 2 * TOK * PACK
         spans = [(g, i * span) for g in range(GROUPS) for i in range(BLOCKS // 2)]
-        early_roots = held([P, 5, span], F32, "early_roots")
-        roots = [early_roots[:, i, :] for i in range(5)]
+        all_roots = held([P, len(spans), span], F32, "all_roots")
+        roots = [all_roots[:, i, :] for i in range(len(spans))]
 
         def root_of(i):
             g, c0 = spans[i]
@@ -146,12 +147,18 @@ def tile_list_damped_grasp_scores_kernel(tc, tab_words, tab_scales, tab2_words, 
             square_b(0, n0)
         for i in range(4):
             root_of(i)
+        square_root(0, EARLY, span)
         square_root(1)
         for n0 in range(0, S, TOK):
             square_b(1, n0)
         for i in (2, 3):
             square_root(i)
         root_of(4)
+        for i in range(5, 8):
+            root_of(i)
+            square_root(i - 1)
+        square_root(7, 0, span // 2)
+        square_root(7, span // 2, span)
 
         w1_codes = held([P, GROUPS, K // PASS, PASS], U32, "w1_codes")
         w1_scale = held([P, GROUPS, K // PASS, PASS], U8, "w1_scale")
@@ -197,7 +204,7 @@ def tile_list_damped_grasp_scores_kernel(tc, tab_words, tab_scales, tab2_words, 
 
         def damped(g, n0):
             cols = slice(n0 * PACK, (n0 + TOK) * PACK)
-            factor = early_damp[:, cols] if g == 0 and cols.stop <= span else damp[:, g, cols]
+            factor = early_damp[:, cols] if g == 0 and cols.stop <= EARLY else damp[:, g, cols]
             nc.vector.tensor_tensor(h_part(g, n0, n0 + TOK).rearrange("p (n t) -> p n t", t=PACK),
                                     a_banks.pop((g, n0))[:].rearrange("p t n -> p n t"),
                                     factor.rearrange("p (n t) -> p n t", t=PACK), ALU.mult)
@@ -244,12 +251,9 @@ def tile_list_damped_grasp_scores_kernel(tc, tab_words, tab_scales, tab2_words, 
         for a in range(K // PASS):
             quantize_w1(0, a, rounded[a])
         load_w1(1, 0)
-        last_rows = w1[PASS:K, PASS:H].rearrange("(p j) c -> p j c", j=PACK)
-        last_raw = [held([P, PACK, PASS // 2], F32, "last_raw%d" % i, tag=tag) for i, tag in enumerate(("w1_raw1", "grouped00"))]
-        for i in range(2):
-            nc.sync.dma_start(last_raw[i][:], last_rows[:, :, i * PASS // 2:(i + 1) * PASS // 2])
-        early_damp = held([P, span], F32, "early_damp", tag="grouped01")
-        nc.vector.tensor_tensor(early_damp[:], roots[0], roots[0], ALU.mult)
+        load_w1(1, 1)
+        early_damp = held([P, EARLY], F32, "early_damp", tag="grouped01")
+        nc.vector.tensor_tensor(early_damp[:], roots[0][:, 0:EARLY], roots[0][:, 0:EARLY], ALU.mult)
         gather(v_codes[0], v_window[0][:].bitcast(U32), list1, 0, S)
         w3_codes = held([P, GROUPS, N], I32, "w3_codes", tag="v_scale_picked")
         nc.sync.dma_start(w3_codes[:], w3_words.rearrange("a p n t -> p a (n t)").bitcast(I32))
@@ -272,20 +276,10 @@ def tile_list_damped_grasp_scores_kernel(tc, tab_words, tab_scales, tab2_words, 
         rounded = [round_w1(1, 0)]
         for n0 in range(0, LATE, TOK):
             damped(0, n0)
-        rounded.append(held([P, PACK, P, PACK], BF16, "grouped11"))
-        last_dst = rounded[1][:].rearrange("p t m j -> p m t j")
-        nc.scalar.copy(last_dst[:, 0:P // 2], last_raw[0][:].rearrange("p j (m t) -> p m t j", t=PACK))
-        late_roots = held([P, 3, span], F32, "late_roots", tag="w1_raw1")
-        roots.extend(late_roots[:, i, :] for i in range(3))
-        for i in range(5, 8):
-            root_of(i)
-            square_root(i - 1)
-        square_root(7, 0, span // 2)
-        square_root(7, span // 2, span)
         quantize_w1(1, 0, rounded[0])
         for n0 in range(0, (BANKS - 1) * TOK, TOK):
             project(1, n0, 0)
-        nc.vector.tensor_copy(last_dst[:, P // 2:P], last_raw[1][:].rearrange("p j (m t) -> p m t j", t=PACK))
+        rounded.append(round_w1(1, 1))
         h_codes[0] = held([P, S], U32, "h_codes0", tag="grouped10")
         quantize_h(0, 0, 512)
         open_scores(0, 256)

@@ -25,7 +25,6 @@ BLOCKS = S // TOK
 BANKS = 3
 LATE = 896
 FIRST = 256
-EARLY = TOK * PACK
 
 
 def tile_list_damped_grasp_scores_kernel(tc, tab_words, tab_scales, tab2_words, tab2_scales, offs, offs2, w1,
@@ -56,8 +55,8 @@ def tile_list_damped_grasp_scores_kernel(tc, tab_words, tab_scales, tab2_words, 
         nc.gpsimd.memset(u_scale_window[:], 0)
         nc.gpsimd.memset(w2_scale_raw[:], 0)
         nc.vector.memset(seed[:, 0:1], 1.0)
-        nc.gpsimd.memset(v_scale_window[:], 0)
-        nc.gpsimd.memset(v_scale[:], 0)
+        nc.vector.memset(v_scale_window[:], 0)
+        nc.vector.memset(v_scale[:], 0)
 
         def load_w1(g, a):
             rows = w1[a * PASS:(a + 1) * PASS, g * PASS:(g + 1) * PASS]
@@ -145,14 +144,17 @@ def tile_list_damped_grasp_scores_kernel(tc, tab_words, tab_scales, tab2_words, 
 
         for n0 in range(0, S, TOK):
             square_b(0, n0)
-        for i in range(4):
+        for i in range(3):
             root_of(i)
-        square_root(0, EARLY, span)
-        square_root(1)
-        for n0 in range(0, S, TOK):
+        for i in (0, 1):
+            square_root(i)
+        for n0 in range(0, S - 2 * TOK, TOK):
             square_b(1, n0)
+        root_of(3)
         for i in (2, 3):
             square_root(i)
+        for n0 in range(S - 2 * TOK, S, TOK):
+            square_b(1, n0)
         root_of(4)
         for i in range(5, 8):
             root_of(i)
@@ -164,7 +166,7 @@ def tile_list_damped_grasp_scores_kernel(tc, tab_words, tab_scales, tab2_words, 
         w1_scale = held([P, GROUPS, K // PASS, PASS], U8, "w1_scale")
 
         def round_w1(g, a):
-            grouped = held([P, PACK, P, PACK], BF16, "grouped%d%d" % (g, a))
+            grouped = held([P, PACK, P, PACK], BF16, "grouped%d%d" % (g, a), tag="v_window1" if (g, a) == (1, 0) else None)
             src = w1_raw[g, a][:].rearrange("p j (m t) -> p m t j", t=PACK)
             dst = grouped[:].rearrange("p t m j -> p m t j")
             if (g, a) in ((1, 0),):
@@ -204,7 +206,7 @@ def tile_list_damped_grasp_scores_kernel(tc, tab_words, tab_scales, tab2_words, 
 
         def damped(g, n0):
             cols = slice(n0 * PACK, (n0 + TOK) * PACK)
-            factor = early_damp[:, cols] if g == 0 and cols.stop <= EARLY else damp[:, g, cols]
+            factor = damp[:, g, cols]
             nc.vector.tensor_tensor(h_part(g, n0, n0 + TOK).rearrange("p (n t) -> p n t", t=PACK),
                                     a_banks.pop((g, n0))[:].rearrange("p t n -> p n t"),
                                     factor.rearrange("p (n t) -> p n t", t=PACK), ALU.mult)
@@ -252,8 +254,6 @@ def tile_list_damped_grasp_scores_kernel(tc, tab_words, tab_scales, tab2_words, 
             quantize_w1(0, a, rounded[a])
         load_w1(1, 0)
         load_w1(1, 1)
-        early_damp = held([P, EARLY], F32, "early_damp", tag="grouped01")
-        nc.vector.tensor_tensor(early_damp[:], roots[0][:, 0:EARLY], roots[0][:, 0:EARLY], ALU.mult)
         gather(v_codes[0], v_window[0][:].bitcast(U32), list1, 0, S)
         w3_codes = held([P, GROUPS, N], I32, "w3_codes", tag="v_scale_picked")
         nc.sync.dma_start(w3_codes[:], w3_words.rearrange("a p n t -> p a (n t)").bitcast(I32))
@@ -280,7 +280,7 @@ def tile_list_damped_grasp_scores_kernel(tc, tab_words, tab_scales, tab2_words, 
         for n0 in range(0, (BANKS - 1) * TOK, TOK):
             project(1, n0, 0)
         rounded.append(round_w1(1, 1))
-        h_codes[0] = held([P, S], U32, "h_codes0", tag="grouped10")
+        h_codes[0] = held([P, S], U32, "h_codes0", tag="v_window1")
         quantize_h(0, 0, 512)
         open_scores(0, 256)
         open_scores(256, 512)

@@ -25,6 +25,7 @@ BLOCKS = S // TOK
 BANKS = 3
 LATE = 896
 FIRST = 256
+EARLY = 2 * TOK * PACK
 
 
 def tile_list_damped_grasp_scores_kernel(tc, tab_words, tab_scales, tab2_words, tab2_scales, offs, offs2, w1,
@@ -44,7 +45,7 @@ def tile_list_damped_grasp_scores_kernel(tc, tab_words, tab_scales, tab2_words, 
         list2 = keep.tile([P, S // 16], U16, name="list2")
         v_window = [held([P, T], I32, "v_window0")]
         v_scale_window = held([P, T // 4], I32, "v_scale_window", tag="v_window1")
-        v_scale = held([P, S // 4], I32, "v_scale")
+        v_scale = [held([P, S // 4], I32, "v_scale%d" % a) for a in range(K // PASS)]
         u_window = held([P, T2], I32, "u_window")
         u_scale_window = held([P, T2 // 4], I32, "u_scale_window")
         w2_raw = held([P, H // 2], I32, "w2_raw")
@@ -56,7 +57,8 @@ def tile_list_damped_grasp_scores_kernel(tc, tab_words, tab_scales, tab2_words, 
         nc.gpsimd.memset(w2_scale_raw[:], 0)
         nc.vector.memset(seed[:, 0:1], 1.0)
         nc.vector.memset(v_scale_window[:], 0)
-        nc.vector.memset(v_scale[:], 0)
+        for plane in v_scale:
+            nc.vector.memset(plane[:], 0)
 
         def load_w1(g, a):
             rows = w1[a * PASS:(a + 1) * PASS, g * PASS:(g + 1) * PASS]
@@ -86,8 +88,8 @@ def tile_list_damped_grasp_scores_kernel(tc, tab_words, tab_scales, tab2_words, 
 
         w2_codes = held([P, 2 * H], U8, "w2_codes")
         w2_scale = held([P, H], U8, "w2_scale")
-        u_scale_first = held([P, S // 2], U8, "u_scale_first")
-        gather(u_scale_first, u_scale_window[:].bitcast(U8), list2, 0, S // 2)
+        u_scale = held([P, S], U8, "u_scale")
+        gather(u_scale, u_scale_window[:].bitcast(U8), list2, 0, S)
         nc.vector.tensor_copy(w2_codes[:].bitcast(U16).rearrange("p (g t m) -> p g t m", g=GROUPS, t=PACK),
                               w2_raw[:].bitcast(U16).rearrange("p (g m t) -> p g t m", g=GROUPS, t=PACK))
         u_first = held([P, FIRST], U32, "u_first")
@@ -96,12 +98,9 @@ def tile_list_damped_grasp_scores_kernel(tc, tab_words, tab_scales, tab2_words, 
             cols = slice(g * PASS, (g + 1) * PASS)
             nc.vector.tensor_copy(w2_scale[:, cols].rearrange("p (t m) -> p t m", t=PACK),
                                   w2_scale_raw[:].bitcast(U8)[:, cols].rearrange("p (m t) -> p t m", t=PACK))
-        u_scale_rest = early.tile([P, S // 2], U8, name="u_scale_rest", align_bytes=64, offset=0)
-        u_rest = early.tile([P, S], U32, name="u_rest", align_bytes=64, offset=S // 2)
+        u_rest = early.tile([P, S], U32, name="u_rest", align_bytes=64, offset=0)
         gather(u_rest, u_window[:].bitcast(U32), list2, FIRST, 2 * FIRST)
-        nc.vector.tensor_copy(u_scale_rest[:], u_scale_window[:].bitcast(U8).indirect(list2[:, S // 32:S // 16]))
-        gather(u_rest, u_window[:].bitcast(U32), list2, 2 * FIRST, 3 * FIRST)
-        gather(u_rest, u_window[:].bitcast(U32), list2, 3 * FIRST, S)
+        gather(u_rest, u_window[:].bitcast(U32), list2, 2 * FIRST, S)
 
         v_scale_picked = held([P, S], U8, "v_scale_picked")
         gather(v_scale_picked, v_scale_window[:].bitcast(U8), list1, 0, S)
@@ -109,7 +108,7 @@ def tile_list_damped_grasp_scores_kernel(tc, tab_words, tab_scales, tab2_words, 
         def place_scale_rows(a):
             for r in range(4):
                 first = 64 * a + 4 * r
-                nc.sync.dma_start(v_scale[4 * a + r:P:32, :], v_scale_picked[:].bitcast(I32)[first:first + 49:16, :])
+                nc.sync.dma_start(v_scale[a][r:P:32, :], v_scale_picked[:].bitcast(I32)[first:first + 49:16, :])
 
         place_scale_rows(0)
         v_window.append(held([P, T], I32, "v_window1"))
@@ -125,7 +124,7 @@ def tile_list_damped_grasp_scores_kernel(tc, tab_words, tab_scales, tab2_words, 
                 m0 = g * PASS + t * P
                 nc.tensor.matmul_mx(out=b_bank[:, t, :], lhsT=w2_codes[:, 2 * m0:2 * (m0 + P)].bitcast(FP4X4),
                                     lhsT_scale=w2_scale[:, m0:m0 + P], rhs=(u_first if n0 < FIRST else u_rest)[:, cols].bitcast(FP8X4),
-                                    rhs_scale=u_scale_first[:, cols] if n0 < S // 2 else u_scale_rest[:, n0 - S // 2:n0 - S // 2 + TOK], start=True, stop=True)
+                                    rhs_scale=u_scale[:, cols], start=True, stop=True)
             nc.scalar.activation(damp[:, g, n0 * PACK:(n0 + TOK) * PACK].rearrange("p (n t) -> p n t", t=PACK),
                                  b_bank[:].rearrange("p t n -> p n t"), ACT.Square)
 
@@ -144,17 +143,15 @@ def tile_list_damped_grasp_scores_kernel(tc, tab_words, tab_scales, tab2_words, 
 
         for n0 in range(0, S, TOK):
             square_b(0, n0)
-        for i in range(3):
-            root_of(i)
         for i in (0, 1):
-            square_root(i)
-        for n0 in range(0, S - 2 * TOK, TOK):
+            root_of(i)
+        square_root(1)
+        for n0 in range(0, S, TOK):
             square_b(1, n0)
-        root_of(3)
         for i in (2, 3):
-            square_root(i)
-        for n0 in range(S - 2 * TOK, S, TOK):
-            square_b(1, n0)
+            root_of(i)
+            square_root(i, 0, span // 2)
+            square_root(i, span // 2, span)
         root_of(4)
         for i in range(5, 8):
             root_of(i)
@@ -196,7 +193,7 @@ def tile_list_damped_grasp_scores_kernel(tc, tab_words, tab_scales, tab2_words, 
                 m_cols = slice(t * P, (t + 1) * P)
                 nc.tensor.matmul_mx(out=a_banks[g, n0][:, t, :], lhsT=w1_codes[:, g, a, m_cols].bitcast(FP8X4),
                                     lhsT_scale=w1_scale[:, g, a, m_cols],
-                                    rhs=v_codes[a][:, cols].bitcast(FP8X4), rhs_scale=v_scale[:].bitcast(U8)[4 * a:P, cols],
+                                    rhs=v_codes[a][:, cols].bitcast(FP8X4), rhs_scale=v_scale[a][:].bitcast(U8)[:, cols],
                                     start=(a == 0 and t == 0), stop=(a == 1 and t == PACK - 1))
 
         def h_part(g, lo, hi):
@@ -206,7 +203,7 @@ def tile_list_damped_grasp_scores_kernel(tc, tab_words, tab_scales, tab2_words, 
 
         def damped(g, n0):
             cols = slice(n0 * PACK, (n0 + TOK) * PACK)
-            factor = damp[:, g, cols]
+            factor = early_damp[:, cols] if g == 0 and cols.stop <= EARLY else damp[:, g, cols]
             nc.vector.tensor_tensor(h_part(g, n0, n0 + TOK).rearrange("p (n t) -> p n t", t=PACK),
                                     a_banks.pop((g, n0))[:].rearrange("p t n -> p n t"),
                                     factor.rearrange("p (n t) -> p n t", t=PACK), ALU.mult)
@@ -255,10 +252,12 @@ def tile_list_damped_grasp_scores_kernel(tc, tab_words, tab_scales, tab2_words, 
         load_w1(1, 0)
         load_w1(1, 1)
         gather(v_codes[0], v_window[0][:].bitcast(U32), list1, 0, S)
+        early_damp = held([P, EARLY], F32, "early_damp", tag="v_window0")
+        nc.vector.tensor_tensor(early_damp[:], roots[0][:, 0:EARLY], roots[0][:, 0:EARLY], ALU.mult)
         w3_codes = held([P, GROUPS, N], I32, "w3_codes", tag="v_scale_picked")
         nc.sync.dma_start(w3_codes[:], w3_words.rearrange("a p n t -> p a (n t)").bitcast(I32))
-        w3_scale = held([P, GROUPS, N // 4], I32, "w3_scale", tag="v_window0")
-        nc.vector.memset(w3_scale[:], 0)
+        w3_scale = held([P, GROUPS, N // 4], I32, "w3_scale", tag="grouped01")
+        nc.gpsimd.memset(w3_scale[:], 0)
         for q in range(4):
             nc.sync.dma_start(w3_scale[q:P:32, :, :],
                               w3_scales[:, q:16:4, :].rearrange("a r n -> r a n").bitcast(I32))
@@ -289,8 +288,8 @@ def tile_list_damped_grasp_scores_kernel(tc, tab_words, tab_scales, tab2_words, 
         for n0 in range(0, (BANKS - 1) * TOK, TOK):
             project(1, n0, 1)
         waiting.extend((1, n0) for n0 in range((BANKS - 1) * TOK, S, TOK))
-        damped(0, 896)
         quantize_h(0, 512, 768)
+        damped(0, 896)
         open_scores(512, 768)
         quantize_h(0, 768, 896)
         open_scores(768, 896)

@@ -22,10 +22,10 @@ PASS = P * PACK
 TOK = 128
 GROUPS = H // PASS
 BLOCKS = S // TOK
-BANKS = 3
+BANKS = 4
 LATE = 896
 FIRST = 256
-EARLY = 2 * TOK * PACK
+AHEAD = 768
 
 
 def tile_list_damped_grasp_scores_kernel(tc, tab_words, tab_scales, tab2_words, tab2_scales, offs, offs2, w1,
@@ -88,8 +88,8 @@ def tile_list_damped_grasp_scores_kernel(tc, tab_words, tab_scales, tab2_words, 
 
         w2_codes = held([P, 2 * H], U8, "w2_codes")
         w2_scale = held([P, H], U8, "w2_scale")
-        u_scale = held([P, S], U8, "u_scale")
-        gather(u_scale, u_scale_window[:].bitcast(U8), list2, 0, S)
+        u_scale_first = held([P, AHEAD], U8, "u_scale_first")
+        gather(u_scale_first, u_scale_window[:].bitcast(U8), list2, 0, AHEAD)
         nc.vector.tensor_copy(w2_codes[:].bitcast(U16).rearrange("p (g t m) -> p g t m", g=GROUPS, t=PACK),
                               w2_raw[:].bitcast(U16).rearrange("p (g m t) -> p g t m", g=GROUPS, t=PACK))
         u_first = held([P, FIRST], U32, "u_first")
@@ -98,9 +98,11 @@ def tile_list_damped_grasp_scores_kernel(tc, tab_words, tab_scales, tab2_words, 
             cols = slice(g * PASS, (g + 1) * PASS)
             nc.vector.tensor_copy(w2_scale[:, cols].rearrange("p (t m) -> p t m", t=PACK),
                                   w2_scale_raw[:].bitcast(U8)[:, cols].rearrange("p (m t) -> p t m", t=PACK))
-        u_rest = early.tile([P, S], U32, name="u_rest", align_bytes=64, offset=0)
+        u_scale_rest = early.tile([P, S - AHEAD], U8, name="u_scale_rest", align_bytes=64, offset=0)
+        u_rest = early.tile([P, S], U32, name="u_rest", align_bytes=64, offset=S // 2)
         gather(u_rest, u_window[:].bitcast(U32), list2, FIRST, 2 * FIRST)
         gather(u_rest, u_window[:].bitcast(U32), list2, 2 * FIRST, S)
+        nc.vector.tensor_copy(u_scale_rest[:], u_scale_window[:].bitcast(U8).indirect(list2[:, AHEAD // 16:S // 16]))
 
         v_scale_picked = held([P, S], U8, "v_scale_picked")
         gather(v_scale_picked, v_scale_window[:].bitcast(U8), list1, 0, S)
@@ -124,7 +126,7 @@ def tile_list_damped_grasp_scores_kernel(tc, tab_words, tab_scales, tab2_words, 
                 m0 = g * PASS + t * P
                 nc.tensor.matmul_mx(out=b_bank[:, t, :], lhsT=w2_codes[:, 2 * m0:2 * (m0 + P)].bitcast(FP4X4),
                                     lhsT_scale=w2_scale[:, m0:m0 + P], rhs=(u_first if n0 < FIRST else u_rest)[:, cols].bitcast(FP8X4),
-                                    rhs_scale=u_scale[:, cols], start=True, stop=True)
+                                    rhs_scale=u_scale_first[:, cols] if n0 < AHEAD else u_scale_rest[:, n0 - AHEAD:n0 - AHEAD + TOK], start=True, stop=True)
             nc.scalar.activation(damp[:, g, n0 * PACK:(n0 + TOK) * PACK].rearrange("p (n t) -> p n t", t=PACK),
                                  b_bank[:].rearrange("p t n -> p n t"), ACT.Square)
 
@@ -143,9 +145,9 @@ def tile_list_damped_grasp_scores_kernel(tc, tab_words, tab_scales, tab2_words, 
 
         for n0 in range(0, S, TOK):
             square_b(0, n0)
-        for i in (0, 1):
-            root_of(i)
-        square_root(1)
+        for step in (root_of, square_root):
+            for i in (0, 1):
+                step(i)
         for n0 in range(0, S, TOK):
             square_b(1, n0)
         for i in (2, 3):
@@ -203,7 +205,7 @@ def tile_list_damped_grasp_scores_kernel(tc, tab_words, tab_scales, tab2_words, 
 
         def damped(g, n0):
             cols = slice(n0 * PACK, (n0 + TOK) * PACK)
-            factor = early_damp[:, cols] if g == 0 and cols.stop <= EARLY else damp[:, g, cols]
+            factor = damp[:, g, cols]
             nc.vector.tensor_tensor(h_part(g, n0, n0 + TOK).rearrange("p (n t) -> p n t", t=PACK),
                                     a_banks.pop((g, n0))[:].rearrange("p t n -> p n t"),
                                     factor.rearrange("p (n t) -> p n t", t=PACK), ALU.mult)
@@ -252,8 +254,6 @@ def tile_list_damped_grasp_scores_kernel(tc, tab_words, tab_scales, tab2_words, 
         load_w1(1, 0)
         load_w1(1, 1)
         gather(v_codes[0], v_window[0][:].bitcast(U32), list1, 0, S)
-        early_damp = held([P, EARLY], F32, "early_damp", tag="v_window0")
-        nc.vector.tensor_tensor(early_damp[:], roots[0][:, 0:EARLY], roots[0][:, 0:EARLY], ALU.mult)
         w3_codes = held([P, GROUPS, N], I32, "w3_codes", tag="v_scale_picked")
         nc.sync.dma_start(w3_codes[:], w3_words.rearrange("a p n t -> p a (n t)").bitcast(I32))
         w3_scale = held([P, GROUPS, N // 4], I32, "w3_scale", tag="grouped01")

@@ -35,7 +35,7 @@ def tile_list_damped_grasp_scores_kernel(tc, tab_words, tab_scales, tab2_words, 
         keep = ctx.enter_context(tc.tile_pool(name="keep", bufs=1))
         early = ctx.enter_context(tc.tile_pool(name="early", bufs=1))
         ring = ctx.enter_context(tc.tile_pool(name="ring", bufs=4))
-        psum_ab = ctx.enter_context(tc.psum_pool(name="psum_ab", bufs=BANKS))
+        psum_ab = ctx.enter_context(tc.psum_pool(name="psum_ab", bufs=1))
         psum_by = ctx.enter_context(tc.psum_pool(name="psum_by", bufs=4))
 
         def held(shape, dtype, name, tag=None):
@@ -119,7 +119,7 @@ def tile_list_damped_grasp_scores_kernel(tc, tab_words, tab_scales, tab2_words, 
 
         damp = held([P, GROUPS, S * PACK], F32, "damp")
 
-        def square_b(g, n0):
+        def multiply_b(g, n0):
             cols = slice(n0, n0 + TOK)
             b_bank = psum_by.tile([P, PACK, TOK], F32, name="b_bank", tag="bank")
             for t in range(PACK):
@@ -127,6 +127,12 @@ def tile_list_damped_grasp_scores_kernel(tc, tab_words, tab_scales, tab2_words, 
                 nc.tensor.matmul_mx(out=b_bank[:, t, :], lhsT=w2_codes[:, 2 * m0:2 * (m0 + P)].bitcast(FP4X4),
                                     lhsT_scale=w2_scale[:, m0:m0 + P], rhs=(u_first if n0 < FIRST else u_rest)[:, cols].bitcast(FP8X4),
                                     rhs_scale=u_scale_first[:, cols] if n0 < AHEAD else u_scale_rest[:, n0 - AHEAD:n0 - AHEAD + TOK], start=True, stop=True)
+            return b_bank
+
+        def square_b(g, n0):
+            square_bank(g, n0, multiply_b(g, n0))
+
+        def square_bank(g, n0, b_bank):
             nc.scalar.activation(damp[:, g, n0 * PACK:(n0 + TOK) * PACK].rearrange("p (n t) -> p n t", t=PACK),
                                  b_bank[:].rearrange("p t n -> p n t"), ACT.Square)
 
@@ -148,12 +154,15 @@ def tile_list_damped_grasp_scores_kernel(tc, tab_words, tab_scales, tab2_words, 
         for step in (root_of, square_root):
             for i in (0, 1):
                 step(i)
-        for n0 in range(0, S, TOK):
+        for n0 in range(0, S // 2, TOK):
             square_b(1, n0)
+        later = [multiply_b(1, n0) for n0 in range(S // 2, S, TOK)]
         for i in (2, 3):
             root_of(i)
             square_root(i, 0, span // 2)
             square_root(i, span // 2, span)
+        for n0, b_bank in zip(range(S // 2, S, TOK), later):
+            square_bank(1, n0, b_bank)
         root_of(4)
         for i in range(5, 8):
             root_of(i)
@@ -186,11 +195,14 @@ def tile_list_damped_grasp_scores_kernel(tc, tab_words, tab_scales, tab2_words, 
         h_bf = held([P, GROUPS, S * PACK], BF16, "h_bf")
         a_banks = {}
         waiting = []
+        bank_of = {}
+        free = list(reversed(range(BANKS)))
 
         def project(g, n0, a):
             cols = slice(n0, n0 + TOK)
             if a == 0:
-                a_banks[g, n0] = psum_ab.tile([P, PACK, TOK], F32, name="a_bank", tag="bank")
+                bank_of[g, n0] = free.pop()
+                a_banks[g, n0] = psum_ab.tile([P, PACK, TOK], F32, name="a_bank", tag="bank%d" % bank_of[g, n0])
             for t in range(PACK):
                 m_cols = slice(t * P, (t + 1) * P)
                 nc.tensor.matmul_mx(out=a_banks[g, n0][:, t, :], lhsT=w1_codes[:, g, a, m_cols].bitcast(FP8X4),
@@ -209,8 +221,9 @@ def tile_list_damped_grasp_scores_kernel(tc, tab_words, tab_scales, tab2_words, 
             nc.vector.tensor_tensor(h_part(g, n0, n0 + TOK).rearrange("p (n t) -> p n t", t=PACK),
                                     a_banks.pop((g, n0))[:].rearrange("p t n -> p n t"),
                                     factor.rearrange("p (n t) -> p n t", t=PACK), ALU.mult)
-            if waiting:
-                ahead = waiting.pop(0)
+            free.append(bank_of[g, n0])
+            ahead = waiting.pop(0) if waiting else None
+            if ahead:
                 project(*ahead, 0)
                 project(*ahead, 1)
 
@@ -271,11 +284,13 @@ def tile_list_damped_grasp_scores_kernel(tc, tab_words, tab_scales, tab2_words, 
 
         for n0 in range(0, BANKS * TOK, TOK):
             project(0, n0, 1)
-        waiting.extend((0, n0) for n0 in range(BANKS * TOK, S, TOK))
+        waiting.extend((0, n0) for n0 in range(BANKS * TOK, LATE, TOK))
+        waiting.extend((None, None, (0, LATE)))
         rounded = [round_w1(1, 0)]
         for n0 in range(0, LATE, TOK):
             damped(0, n0)
         quantize_w1(1, 0, rounded[0])
+        free.reverse()
         for n0 in range(0, (BANKS - 1) * TOK, TOK):
             project(1, n0, 0)
         rounded.append(round_w1(1, 1))

@@ -34,6 +34,7 @@ def tile_list_damped_grasp_scores_kernel(tc, tab_words, tab_scales, tab2_words, 
     with ExitStack() as ctx:
         keep = ctx.enter_context(tc.tile_pool(name="keep", bufs=1))
         early = ctx.enter_context(tc.tile_pool(name="early", bufs=1))
+        late = ctx.enter_context(tc.tile_pool(name="late", bufs=1))
         ring = ctx.enter_context(tc.tile_pool(name="ring", bufs=4))
         psum_ab = ctx.enter_context(tc.psum_pool(name="psum_ab", bufs=1))
         psum_by = ctx.enter_context(tc.psum_pool(name="psum_by", bufs=4))
@@ -51,6 +52,7 @@ def tile_list_damped_grasp_scores_kernel(tc, tab_words, tab_scales, tab2_words, 
         w2_raw = held([P, H // 2], I32, "w2_raw")
         w2_scale_raw = early.tile([P, H // 4], I32, name="w2_scale_raw", align_bytes=64, offset=0)
         w1_raw = {}
+        w1_last = []
 
         seed = held([P, 16], F32, "seed")
         nc.gpsimd.memset(u_scale_window[:], 0)
@@ -62,7 +64,16 @@ def tile_list_damped_grasp_scores_kernel(tc, tab_words, tab_scales, tab2_words, 
 
         def load_w1(g, a):
             rows = w1[a * PASS:(a + 1) * PASS, g * PASS:(g + 1) * PASS]
-            w1_raw[g, a] = held([P, PACK, PASS], F32, "w1_raw%d%d" % (g, a), tag="w1_raw%d" % a)
+            if (g, a) == (1, 1):
+                for part, at in enumerate((2048, 8192)):
+                    w1_last.append(late.tile([P, PACK, PASS // 2], F32, name="w1_last%d" % part, align_bytes=64, offset=at))
+                    nc.sync.dma_start(w1_last[part][:],
+                                      rows[:, part * PASS // 2:(part + 1) * PASS // 2].rearrange("(p j) c -> p j c", j=PACK))
+                return
+            if a == 1:
+                w1_raw[g, a] = late.tile([P, PACK, PASS], F32, name="w1_raw01", align_bytes=64, offset=4096)
+            else:
+                w1_raw[g, a] = held([P, PACK, PASS], F32, "w1_raw%d%d" % (g, a), tag="w1_raw%d" % a)
             nc.sync.dma_start(w1_raw[g, a][:], rows.rearrange("(p j) c -> p j c", j=PACK))
 
         def words_of(packed):
@@ -138,11 +149,14 @@ def tile_list_damped_grasp_scores_kernel(tc, tab_words, tab_scales, tab2_words, 
 
         span = 2 * TOK * PACK
         spans = [(g, i * span) for g in range(GROUPS) for i in range(BLOCKS // 2)]
-        all_roots = held([P, len(spans), span], F32, "all_roots")
-        roots = [all_roots[:, i, :] for i in range(len(spans))]
+        all_roots = held([P, len(spans) // 2, span], F32, "all_roots")
+        roots = [all_roots[:, i, :] for i in range(len(spans) // 2)]
 
         def root_of(i):
             g, c0 = spans[i]
+            if g == 1:
+                root = late.tile([P, span], F32, name="root%d" % i, align_bytes=64, offset=(i % 2) * 4096)
+                roots.append(root[:])
             nc.scalar.activation(roots[i], damp[:, g, c0:c0 + span], ACT.Abs_reciprocal_sqrt, bias=seed[:, 8:9])
 
         def square_root(i, lo=0, hi=span):
@@ -163,20 +177,26 @@ def tile_list_damped_grasp_scores_kernel(tc, tab_words, tab_scales, tab2_words, 
             square_root(i, span // 2, span)
         for n0, b_bank in zip(range(S // 2, S, TOK), later):
             square_bank(1, n0, b_bank)
-        root_of(4)
-        for i in range(5, 8):
-            root_of(i)
-            square_root(i - 1)
-        square_root(7, 0, span // 2)
-        square_root(7, span // 2, span)
+
+        def late_factors():
+            root_of(4)
+            for i in range(5, 8):
+                root_of(i)
+                square_root(i - 1)
+            square_root(7, 0, span // 2)
+            square_root(7, span // 2, span)
 
         w1_codes = held([P, GROUPS, K // PASS, PASS], U32, "w1_codes")
         w1_scale = held([P, GROUPS, K // PASS, PASS], U8, "w1_scale")
 
         def round_w1(g, a):
             grouped = held([P, PACK, P, PACK], BF16, "grouped%d%d" % (g, a), tag="v_window1" if (g, a) == (1, 0) else None)
-            src = w1_raw[g, a][:].rearrange("p j (m t) -> p m t j", t=PACK)
             dst = grouped[:].rearrange("p t m j -> p m t j")
+            if (g, a) == (1, 1):
+                for part, move in enumerate((nc.scalar.copy, nc.vector.tensor_copy)):
+                    move(dst[:, part * P // 2:(part + 1) * P // 2], w1_last[part][:].rearrange("p j (m t) -> p m t j", t=PACK))
+                return grouped
+            src = w1_raw[g, a][:].rearrange("p j (m t) -> p m t j", t=PACK)
             if (g, a) in ((1, 0),):
                 for m0 in range(0, P, 32):
                     nc.gpsimd.tensor_scalar(dst[:, m0:m0 + 32], src[:, m0:m0 + 32], 1.0, 0.0, ALU.mult, ALU.add)
@@ -294,6 +314,7 @@ def tile_list_damped_grasp_scores_kernel(tc, tab_words, tab_scales, tab2_words, 
         for n0 in range(0, (BANKS - 1) * TOK, TOK):
             project(1, n0, 0)
         rounded.append(round_w1(1, 1))
+        late_factors()
         h_codes[0] = held([P, S], U32, "h_codes0", tag="v_window1")
         quantize_h(0, 0, 512)
         open_scores(0, 256)

@@ -26,6 +26,8 @@ BANKS = 4
 LATE = 896
 FIRST = 256
 AHEAD = 768
+SHARE = 64
+HALF = S // 2
 
 
 def tile_list_damped_grasp_scores_kernel(tc, tab_words, tab_scales, tab2_words, tab2_scales, offs, offs2, w1,
@@ -35,7 +37,8 @@ def tile_list_damped_grasp_scores_kernel(tc, tab_words, tab_scales, tab2_words, 
         keep = ctx.enter_context(tc.tile_pool(name="keep", bufs=1))
         early = ctx.enter_context(tc.tile_pool(name="early", bufs=1))
         late = ctx.enter_context(tc.tile_pool(name="late", bufs=1))
-        ring = ctx.enter_context(tc.tile_pool(name="ring", bufs=4))
+        tail = ctx.enter_context(tc.tile_pool(name="tail", bufs=1))
+        ring = ctx.enter_context(tc.tile_pool(name="ring", bufs=5))
         psum_ab = ctx.enter_context(tc.psum_pool(name="psum_ab", bufs=1))
         psum_by = ctx.enter_context(tc.psum_pool(name="psum_by", bufs=4))
 
@@ -45,7 +48,7 @@ def tile_list_damped_grasp_scores_kernel(tc, tab_words, tab_scales, tab2_words, 
         list1 = keep.tile([P, S // 16], U16, name="list1")
         list2 = keep.tile([P, S // 16], U16, name="list2")
         v_window = [held([P, T], I32, "v_window0")]
-        v_scale_window = held([P, T // 4], I32, "v_scale_window", tag="v_window1")
+        v_scale_window = tail.tile([P, T // 4], I32, name="v_scale_window", align_bytes=64, offset=0)
         v_scale = [held([P, S // 4], I32, "v_scale%d" % a) for a in range(K // PASS)]
         u_window = held([P, T2], I32, "u_window")
         u_scale_window = held([P, T2 // 4], I32, "u_scale_window")
@@ -65,10 +68,9 @@ def tile_list_damped_grasp_scores_kernel(tc, tab_words, tab_scales, tab2_words, 
         def load_w1(g, a):
             rows = w1[a * PASS:(a + 1) * PASS, g * PASS:(g + 1) * PASS]
             if (g, a) == (1, 1):
-                for part, at in enumerate((2048, 8192)):
-                    w1_last.append(late.tile([P, PACK, PASS // 2], F32, name="w1_last%d" % part, align_bytes=64, offset=at))
-                    nc.sync.dma_start(w1_last[part][:],
-                                      rows[:, part * PASS // 2:(part + 1) * PASS // 2].rearrange("(p j) c -> p j c", j=PACK))
+                for part, (at, lo, hi) in enumerate(((2048, 0, SHARE), (8192, SHARE, P))):
+                    w1_last.append(late.tile([P, PACK, (hi - lo) * PACK], F32, name="w1_last%d" % part, align_bytes=64, offset=at))
+                    nc.sync.dma_start(w1_last[part][:], rows[:, lo * PACK:hi * PACK].rearrange("(p j) c -> p j c", j=PACK))
                 return
             if a == 1:
                 w1_raw[g, a] = late.tile([P, PACK, PASS], F32, name="w1_raw01", align_bytes=64, offset=4096)
@@ -124,7 +126,7 @@ def tile_list_damped_grasp_scores_kernel(tc, tab_words, tab_scales, tab2_words, 
                 nc.sync.dma_start(v_scale[a][r:P:32, :], v_scale_picked[:].bitcast(I32)[first:first + 49:16, :])
 
         place_scale_rows(0)
-        v_window.append(held([P, T], I32, "v_window1"))
+        v_window.append(tail.tile([P, T], I32, name="v_window1", align_bytes=64, offset=0))
         nc.sync.dma_start(v_window[1][:], words_of(tab_words[1]))
         place_scale_rows(1)
 
@@ -152,12 +154,12 @@ def tile_list_damped_grasp_scores_kernel(tc, tab_words, tab_scales, tab2_words, 
         all_roots = held([P, len(spans) // 2, span], F32, "all_roots")
         roots = [all_roots[:, i, :] for i in range(len(spans) // 2)]
 
-        def root_of(i):
+        def root_of(i, lo=0, hi=span):
             g, c0 = spans[i]
-            if g == 1:
+            if g == 1 and lo == 0:
                 root = late.tile([P, span], F32, name="root%d" % i, align_bytes=64, offset=(i % 2) * 4096)
                 roots.append(root[:])
-            nc.scalar.activation(roots[i], damp[:, g, c0:c0 + span], ACT.Abs_reciprocal_sqrt, bias=seed[:, 8:9])
+            nc.scalar.activation(roots[i][:, lo:hi], damp[:, g, c0 + lo:c0 + hi], ACT.Abs_reciprocal_sqrt, bias=seed[:, 8:9])
 
         def square_root(i, lo=0, hi=span):
             g, c0 = spans[i]
@@ -174,27 +176,32 @@ def tile_list_damped_grasp_scores_kernel(tc, tab_words, tab_scales, tab2_words, 
         for i in (2, 3):
             root_of(i)
             square_root(i, 0, span // 2)
-            square_root(i, span // 2, span)
+            if i == 2:
+                square_root(i, span // 2, span)
         for n0, b_bank in zip(range(S // 2, S, TOK), later):
             square_bank(1, n0, b_bank)
 
         def late_factors():
-            root_of(4)
-            for i in range(5, 8):
-                root_of(i)
-                square_root(i - 1)
-            square_root(7, 0, span // 2)
-            square_root(7, span // 2, span)
+            for step in (root_of, square_root):
+                for i in (4, 5):
+                    step(i)
+            for i in (6, 7):
+                for step in (root_of, square_root):
+                    step(i, 0, span // 2)
+                    step(i, span // 2, span)
 
         w1_codes = held([P, GROUPS, K // PASS, PASS], U32, "w1_codes")
         w1_scale = held([P, GROUPS, K // PASS, PASS], U8, "w1_scale")
 
         def round_w1(g, a):
-            grouped = held([P, PACK, P, PACK], BF16, "grouped%d%d" % (g, a), tag="v_window1" if (g, a) == (1, 0) else None)
+            if (g, a) == (1, 0):
+                grouped = tail.tile([P, PACK, P, PACK], BF16, name="grouped10", align_bytes=64, offset=0)
+            else:
+                grouped = held([P, PACK, P, PACK], BF16, "grouped%d%d" % (g, a))
             dst = grouped[:].rearrange("p t m j -> p m t j")
             if (g, a) == (1, 1):
-                for part, move in enumerate((nc.scalar.copy, nc.vector.tensor_copy)):
-                    move(dst[:, part * P // 2:(part + 1) * P // 2], w1_last[part][:].rearrange("p j (m t) -> p m t j", t=PACK))
+                for part, (move, lo, hi) in enumerate(((nc.scalar.copy, 0, SHARE), (nc.vector.tensor_copy, SHARE, P))):
+                    move(dst[:, lo:hi], w1_last[part][:].rearrange("p j (m t) -> p m t j", t=PACK))
                 return grouped
             src = w1_raw[g, a][:].rearrange("p j (m t) -> p m t j", t=PACK)
             if (g, a) in ((1, 0),):
@@ -209,7 +216,14 @@ def tile_list_damped_grasp_scores_kernel(tc, tab_words, tab_scales, tab2_words, 
                                   in_=grouped[:].rearrange("p t m j -> p (t m j)"))
 
         v_codes = [held([P, S], U32, "v_codes%d" % a) for a in range(K // PASS)]
-        h_codes = {1: held([P, S], U32, "h_codes1")}
+        h_codes = {}
+        h_codes1 = held([P, S], U32, "h_codes1")
+        for half in range(2):
+            h_codes[1, half] = h_codes1[:, half * HALF:(half + 1) * HALF]
+
+        def codes_of(g, lo, hi):
+            return h_codes[g, lo // HALF][:, lo % HALF:lo % HALF + hi - lo].bitcast(FP8X4)
+
         h_scale = held([P, GROUPS, S], U8, "h_scale")
 
         h_bf = held([P, GROUPS, S * PACK], BF16, "h_bf")
@@ -231,13 +245,11 @@ def tile_list_damped_grasp_scores_kernel(tc, tab_words, tab_scales, tab2_words, 
                                     start=(a == 0 and t == 0), stop=(a == 1 and t == PACK - 1))
 
         def h_part(g, lo, hi):
-            if g == 0 and lo >= LATE:
-                return h_late[:, (lo - LATE) * PACK:(hi - LATE) * PACK]
             return h_bf[:, g, lo * PACK:hi * PACK]
 
         def damped(g, n0):
             cols = slice(n0 * PACK, (n0 + TOK) * PACK)
-            factor = damp[:, g, cols]
+            factor = factor_late[:] if (g, n0) == (0, LATE) else damp[:, g, cols]
             nc.vector.tensor_tensor(h_part(g, n0, n0 + TOK).rearrange("p (n t) -> p n t", t=PACK),
                                     a_banks.pop((g, n0))[:].rearrange("p t n -> p n t"),
                                     factor.rearrange("p (n t) -> p n t", t=PACK), ALU.mult)
@@ -248,12 +260,12 @@ def tile_list_damped_grasp_scores_kernel(tc, tab_words, tab_scales, tab2_words, 
                 project(*ahead, 1)
 
         def quantize_h(g, lo, hi):
-            nc.vector.quantize_mx(out=h_codes[g][:, lo:hi].bitcast(FP8X4), scales=h_scale[:, g, lo:hi], in_=h_part(g, lo, hi))
+            nc.vector.quantize_mx(out=codes_of(g, lo, hi), scales=h_scale[:, g, lo:hi], in_=h_part(g, lo, hi))
 
         def score_pass(y, c, g, lo, hi, start, stop):
             nc.tensor.matmul_mx(out=y, lhsT=w3_codes[:, g, c * P:(c + 1) * P].bitcast(FP8X4),
                                 lhsT_scale=w3_scale[:, g, :].bitcast(U8)[:, c * P:(c + 1) * P],
-                                rhs=h_codes[g][:, lo:hi].bitcast(FP8X4), rhs_scale=h_scale[:, g, lo:hi],
+                                rhs=codes_of(g, lo, hi), rhs_scale=h_scale[:, g, lo:hi],
                                 start=start, stop=stop)
 
         y_banks = {}
@@ -269,10 +281,15 @@ def tile_list_damped_grasp_scores_kernel(tc, tab_words, tab_scales, tab2_words, 
                 y_bank = y_banks.pop(lo)
                 for c in range(N // P):
                     score_pass(y_bank[:, c, :], c, 1, lo, hi, False, c == N // P - 1)
+                if hi == LATE:
+                    quantize_h(1, LATE, S)
                 for c in range(N // P):
-                    nc.scalar.activation(y_sb[:, c, :], y_bank[:, c, :], ACT.Identity, bias=bias_sb[:, c:c + 1])
+                    if hi == LATE:
+                        nc.vector.tensor_scalar(y_sb[:, c, :], y_bank[:, c, :], bias_sb[:, c:c + 1], None, ALU.add)
+                    else:
+                        nc.scalar.activation(y_sb[:, c, :], y_bank[:, c, :], ACT.Identity, bias=bias_sb[:, c:c + 1])
             else:
-                y_last = [psum_by.tile([P, hi - lo], F32, name="y_last%d" % c, tag="bank") for c in range(N // P)]
+                y_last = [psum_ab.tile([P, hi - lo], F32, name="y_last%d" % c, tag="bank%d" % free[c]) for c in range(N // P)]
                 for g in range(GROUPS):
                     for c in range(N // P):
                         score_pass(y_last[c][:], c, g, lo, hi, g == 0, g == GROUPS - 1)
@@ -305,37 +322,39 @@ def tile_list_damped_grasp_scores_kernel(tc, tab_words, tab_scales, tab2_words, 
         for n0 in range(0, BANKS * TOK, TOK):
             project(0, n0, 1)
         waiting.extend((0, n0) for n0 in range(BANKS * TOK, LATE, TOK))
-        waiting.extend((None, None, (0, LATE)))
+        waiting.extend((None, (0, LATE)))
+        factor_late = tail.tile([P, span // 2], F32, name="factor_late", align_bytes=64, offset=4096)
+        nc.gpsimd.tensor_tensor(factor_late[:], roots[3][:, span // 2:], roots[3][:, span // 2:], ALU.mult)
         rounded = [round_w1(1, 0)]
-        for n0 in range(0, LATE, TOK):
+        for n0 in range(0, S, TOK):
             damped(0, n0)
         quantize_w1(1, 0, rounded[0])
         free.reverse()
-        for n0 in range(0, (BANKS - 1) * TOK, TOK):
+        for n0 in range(0, BANKS * TOK, TOK):
             project(1, n0, 0)
         rounded.append(round_w1(1, 1))
         late_factors()
-        h_codes[0] = held([P, S], U32, "h_codes0", tag="v_window1")
+        first_codes = tail.tile([P, HALF], U32, name="h_codes00", align_bytes=64, offset=0)
+        h_codes[0, 0] = first_codes[:]
         quantize_h(0, 0, 512)
         open_scores(0, 256)
         open_scores(256, 512)
         quantize_w1(1, 1, rounded[1])
-        h_late = held([P, TOK * PACK], BF16, "h_late", tag="grouped11")
-        for n0 in range(0, (BANKS - 1) * TOK, TOK):
+        second_codes = held([P, HALF], U32, "h_codes01", tag="grouped11")
+        h_codes[0, 1] = second_codes[:]
+        for n0 in range(0, BANKS * TOK, TOK):
             project(1, n0, 1)
-        waiting.extend((1, n0) for n0 in range((BANKS - 1) * TOK, S, TOK))
-        quantize_h(0, 512, 768)
-        damped(0, 896)
+        waiting.extend((1, n0) for n0 in range(BANKS * TOK, S, TOK))
+        quantize_h(0, 512, 1024)
         open_scores(512, 768)
-        quantize_h(0, 768, 896)
         open_scores(768, 896)
         damped(1, 0)
-        quantize_h(0, 896, 1024)
         chunks = ((0, 256), (256, 512), (512, 768), (768, 896), (896, 1024))
         done = 128
         for lo, hi in chunks:
             while done < min(hi + TOK, S):
                 damped(1, done)
                 done += TOK
-            quantize_h(1, lo, hi)
+            if hi < S:
+                quantize_h(1, lo, hi)
             scores(lo, hi)

@@ -26,7 +26,7 @@ BANKS = 4
 LATE = 896
 FIRST = 256
 AHEAD = 768
-SHARE = 64
+SHARE = 48
 HALF = S // 2
 
 
@@ -176,8 +176,7 @@ def tile_list_damped_grasp_scores_kernel(tc, tab_words, tab_scales, tab2_words, 
         for i in (2, 3):
             root_of(i)
             square_root(i, 0, span // 2)
-            if i == 2:
-                square_root(i, span // 2, span)
+            square_root(i, span // 2, span)
         for n0, b_bank in zip(range(S // 2, S, TOK), later):
             square_bank(1, n0, b_bank)
 
@@ -249,7 +248,7 @@ def tile_list_damped_grasp_scores_kernel(tc, tab_words, tab_scales, tab2_words, 
 
         def damped(g, n0):
             cols = slice(n0 * PACK, (n0 + TOK) * PACK)
-            factor = factor_late[:] if (g, n0) == (0, LATE) else damp[:, g, cols]
+            factor = damp[:, g, cols]
             nc.vector.tensor_tensor(h_part(g, n0, n0 + TOK).rearrange("p (n t) -> p n t", t=PACK),
                                     a_banks.pop((g, n0))[:].rearrange("p t n -> p n t"),
                                     factor.rearrange("p (n t) -> p n t", t=PACK), ALU.mult)
@@ -323,8 +322,6 @@ def tile_list_damped_grasp_scores_kernel(tc, tab_words, tab_scales, tab2_words, 
             project(0, n0, 1)
         waiting.extend((0, n0) for n0 in range(BANKS * TOK, LATE, TOK))
         waiting.extend((None, (0, LATE)))
-        factor_late = tail.tile([P, span // 2], F32, name="factor_late", align_bytes=64, offset=4096)
-        nc.gpsimd.tensor_tensor(factor_late[:], roots[3][:, span // 2:], roots[3][:, span // 2:], ALU.mult)
         rounded = [round_w1(1, 0)]
         for n0 in range(0, S, TOK):
             damped(0, n0)

@@ -203,7 +203,7 @@ def tile_list_damped_grasp_scores_kernel(tc, tab_words, tab_scales, tab2_words, 
                     move(dst[:, lo:hi], w1_last[part][:].rearrange("p j (m t) -> p m t j", t=PACK))
                 return grouped
             src = w1_raw[g, a][:].rearrange("p j (m t) -> p m t j", t=PACK)
-            if (g, a) in ((1, 0),):
+            if a == 0:
                 for m0 in range(0, P, 32):
                     nc.gpsimd.tensor_scalar(dst[:, m0:m0 + 32], src[:, m0:m0 + 32], 1.0, 0.0, ALU.mult, ALU.add)
             else:

@@ -167,9 +167,9 @@ def tile_list_damped_grasp_scores_kernel(tc, tab_words, tab_scales, tab2_words, 
 
         for n0 in range(0, S, TOK):
             square_b(0, n0)
-        for step in (root_of, square_root):
-            for i in (0, 1):
-                step(i)
+        for i in (0, 1):
+            root_of(i)
+        square_root(1)
         for n0 in range(0, S // 2, TOK):
             square_b(1, n0)
         later = [multiply_b(1, n0) for n0 in range(S // 2, S, TOK)]
@@ -248,7 +248,7 @@ def tile_list_damped_grasp_scores_kernel(tc, tab_words, tab_scales, tab2_words, 
 
         def damped(g, n0):
             cols = slice(n0 * PACK, (n0 + TOK) * PACK)
-            factor = damp[:, g, cols]
+            factor = first_factor[:, cols] if g == 0 and n0 * PACK < span else damp[:, g, cols]
             nc.vector.tensor_tensor(h_part(g, n0, n0 + TOK).rearrange("p (n t) -> p n t", t=PACK),
                                     a_banks.pop((g, n0))[:].rearrange("p t n -> p n t"),
                                     factor.rearrange("p (n t) -> p n t", t=PACK), ALU.mult)
@@ -303,6 +303,8 @@ def tile_list_damped_grasp_scores_kernel(tc, tab_words, tab_scales, tab2_words, 
         load_w1(1, 0)
         load_w1(1, 1)
         gather(v_codes[0], v_window[0][:].bitcast(U32), list1, 0, S)
+        first_factor = held([P, span], F32, "first_factor", tag="v_window0")
+        nc.vector.tensor_tensor(first_factor[:], roots[0], roots[0], ALU.mult)
         w3_codes = held([P, GROUPS, N], I32, "w3_codes", tag="v_scale_picked")
         nc.sync.dma_start(w3_codes[:], w3_words.rearrange("a p n t -> p a (n t)").bitcast(I32))
         w3_scale = held([P, GROUPS, N // 4], I32, "w3_scale", tag="grouped01")

@@ -26,7 +26,7 @@ BANKS = 4
 LATE = 896
 FIRST = 256
 AHEAD = 768
-SHARE = 48
+SHARE = 64
 HALF = S // 2
 
 
@@ -169,7 +169,6 @@ def tile_list_damped_grasp_scores_kernel(tc, tab_words, tab_scales, tab2_words, 
             square_b(0, n0)
         for i in (0, 1):
             root_of(i)
-        square_root(1)
         for n0 in range(0, S // 2, TOK):
             square_b(1, n0)
         later = [multiply_b(1, n0) for n0 in range(S // 2, S, TOK)]
@@ -204,8 +203,10 @@ def tile_list_damped_grasp_scores_kernel(tc, tab_words, tab_scales, tab2_words, 
                 return grouped
             src = w1_raw[g, a][:].rearrange("p j (m t) -> p m t j", t=PACK)
             if a == 0:
-                for m0 in range(0, P, 32):
+                for m0 in range(0, SHARE if g else P, 32):
                     nc.gpsimd.tensor_scalar(dst[:, m0:m0 + 32], src[:, m0:m0 + 32], 1.0, 0.0, ALU.mult, ALU.add)
+                if g:
+                    nc.scalar.copy(dst[:, SHARE:P], src[:, SHARE:P])
             else:
                 nc.vector.tensor_copy(dst, src)
             return grouped
@@ -248,7 +249,10 @@ def tile_list_damped_grasp_scores_kernel(tc, tab_words, tab_scales, tab2_words, 
 
         def damped(g, n0):
             cols = slice(n0 * PACK, (n0 + TOK) * PACK)
-            factor = first_factor[:, cols] if g == 0 and n0 * PACK < span else damp[:, g, cols]
+            if g == 0 and n0 * PACK < len(factors) * span:
+                factor = factors[cols.start // span][:, cols.start % span:cols.start % span + TOK * PACK]
+            else:
+                factor = damp[:, g, cols]
             nc.vector.tensor_tensor(h_part(g, n0, n0 + TOK).rearrange("p (n t) -> p n t", t=PACK),
                                     a_banks.pop((g, n0))[:].rearrange("p t n -> p n t"),
                                     factor.rearrange("p (n t) -> p n t", t=PACK), ALU.mult)
@@ -300,11 +304,13 @@ def tile_list_damped_grasp_scores_kernel(tc, tab_words, tab_scales, tab2_words, 
         rounded = [round_w1(0, a) for a in range(K // PASS)]
         for a in range(K // PASS):
             quantize_w1(0, a, rounded[a])
+        factors = [held([P, span], F32, "factor0", tag="grouped00")]
+        nc.vector.tensor_tensor(factors[0][:], roots[0], roots[0], ALU.mult)
         load_w1(1, 0)
         load_w1(1, 1)
         gather(v_codes[0], v_window[0][:].bitcast(U32), list1, 0, S)
-        first_factor = held([P, span], F32, "first_factor", tag="v_window0")
-        nc.vector.tensor_tensor(first_factor[:], roots[0], roots[0], ALU.mult)
+        factors.append(held([P, span], F32, "factor1", tag="v_window0"))
+        nc.vector.tensor_tensor(factors[1][:], roots[1], roots[1], ALU.mult)
         w3_codes = held([P, GROUPS, N], I32, "w3_codes", tag="v_scale_picked")
         nc.sync.dma_start(w3_codes[:], w3_words.rearrange("a p n t -> p a (n t)").bitcast(I32))
         w3_scale = held([P, GROUPS, N // 4], I32, "w3_scale", tag="grouped01")

@@ -26,7 +26,9 @@ BANKS = 4
 LATE = 896
 FIRST = 256
 AHEAD = 768
-SHARE = 64
+SHARE = 48
+ON_GPSIMD = 96
+ON_VECTOR = 3 * TOK * PACK
 HALF = S // 2
 
 
@@ -169,6 +171,7 @@ def tile_list_damped_grasp_scores_kernel(tc, tab_words, tab_scales, tab2_words, 
             square_b(0, n0)
         for i in (0, 1):
             root_of(i)
+        square_root(1, span // 2, span)
         for n0 in range(0, S // 2, TOK):
             square_b(1, n0)
         later = [multiply_b(1, n0) for n0 in range(S // 2, S, TOK)]
@@ -203,10 +206,10 @@ def tile_list_damped_grasp_scores_kernel(tc, tab_words, tab_scales, tab2_words, 
                 return grouped
             src = w1_raw[g, a][:].rearrange("p j (m t) -> p m t j", t=PACK)
             if a == 0:
-                for m0 in range(0, SHARE if g else P, 32):
+                for m0 in range(0, ON_GPSIMD if g else P, 32):
                     nc.gpsimd.tensor_scalar(dst[:, m0:m0 + 32], src[:, m0:m0 + 32], 1.0, 0.0, ALU.mult, ALU.add)
                 if g:
-                    nc.scalar.copy(dst[:, SHARE:P], src[:, SHARE:P])
+                    nc.scalar.copy(dst[:, ON_GPSIMD:P], src[:, ON_GPSIMD:P])
             else:
                 nc.vector.tensor_copy(dst, src)
             return grouped
@@ -249,10 +252,7 @@ def tile_list_damped_grasp_scores_kernel(tc, tab_words, tab_scales, tab2_words, 
 
         def damped(g, n0):
             cols = slice(n0 * PACK, (n0 + TOK) * PACK)
-            if g == 0 and n0 * PACK < len(factors) * span:
-                factor = factors[cols.start // span][:, cols.start % span:cols.start % span + TOK * PACK]
-            else:
-                factor = damp[:, g, cols]
+            factor = first_factors[:, cols] if g == 0 and cols.start < ON_VECTOR else damp[:, g, cols]
             nc.vector.tensor_tensor(h_part(g, n0, n0 + TOK).rearrange("p (n t) -> p n t", t=PACK),
                                     a_banks.pop((g, n0))[:].rearrange("p t n -> p n t"),
                                     factor.rearrange("p (n t) -> p n t", t=PACK), ALU.mult)
@@ -304,13 +304,12 @@ def tile_list_damped_grasp_scores_kernel(tc, tab_words, tab_scales, tab2_words, 
         rounded = [round_w1(0, a) for a in range(K // PASS)]
         for a in range(K // PASS):
             quantize_w1(0, a, rounded[a])
-        factors = [held([P, span], F32, "factor0", tag="grouped00")]
-        nc.vector.tensor_tensor(factors[0][:], roots[0], roots[0], ALU.mult)
         load_w1(1, 0)
         load_w1(1, 1)
         gather(v_codes[0], v_window[0][:].bitcast(U32), list1, 0, S)
-        factors.append(held([P, span], F32, "factor1", tag="v_window0"))
-        nc.vector.tensor_tensor(factors[1][:], roots[1], roots[1], ALU.mult)
+        first_factors = held([P, ON_VECTOR], F32, "first_factors", tag="v_window0")
+        first_roots = all_roots[:].rearrange("p i n -> p (i n)")[:, 0:ON_VECTOR]
+        nc.vector.tensor_tensor(first_factors[:], first_roots, first_roots, ALU.mult)
         w3_codes = held([P, GROUPS, N], I32, "w3_codes", tag="v_scale_picked")
         nc.sync.dma_start(w3_codes[:], w3_words.rearrange("a p n t -> p a (n t)").bitcast(I32))
         w3_scale = held([P, GROUPS, N // 4], I32, "w3_scale", tag="grouped01")

@@ -26,7 +26,7 @@ BANKS = 4
 LATE = 896
 FIRST = 256
 AHEAD = 768
-SHARE = 48
+SHARE = 80
 ON_GPSIMD = 96
 ON_VECTOR = 3 * TOK * PACK
 HALF = S // 2
@@ -70,7 +70,7 @@ def tile_list_damped_grasp_scores_kernel(tc, tab_words, tab_scales, tab2_words, 
         def load_w1(g, a):
             rows = w1[a * PASS:(a + 1) * PASS, g * PASS:(g + 1) * PASS]
             if (g, a) == (1, 1):
-                for part, (at, lo, hi) in enumerate(((2048, 0, SHARE), (8192, SHARE, P))):
+                for part, (at, lo, hi) in enumerate(((7168, 0, SHARE), (4096, SHARE, P))):
                     w1_last.append(late.tile([P, PACK, (hi - lo) * PACK], F32, name="w1_last%d" % part, align_bytes=64, offset=at))
                     nc.sync.dma_start(w1_last[part][:], rows[:, lo * PACK:hi * PACK].rearrange("(p j) c -> p j c", j=PACK))
                 return
@@ -156,16 +156,21 @@ def tile_list_damped_grasp_scores_kernel(tc, tab_words, tab_scales, tab2_words, 
         all_roots = held([P, len(spans) // 2, span], F32, "all_roots")
         roots = [all_roots[:, i, :] for i in range(len(spans) // 2)]
 
+        late_factor = []
+
         def root_of(i, lo=0, hi=span):
             g, c0 = spans[i]
             if g == 1 and lo == 0:
-                root = late.tile([P, span], F32, name="root%d" % i, align_bytes=64, offset=(i % 2) * 4096)
+                root = late.tile([P, span], F32, name="root%d" % i, align_bytes=64, offset=(i % 2) * 11264)
                 roots.append(root[:])
             nc.scalar.activation(roots[i][:, lo:hi], damp[:, g, c0 + lo:c0 + hi], ACT.Abs_reciprocal_sqrt, bias=seed[:, 8:9])
 
         def square_root(i, lo=0, hi=span):
             g, c0 = spans[i]
-            nc.scalar.activation(damp[:, g, c0 + lo:c0 + hi], roots[i][:, lo:hi], ACT.Square)
+            if i == 4:
+                late_factor.append(late.tile([P, span], F32, name="factor4", align_bytes=64, offset=7168))
+            dst = late_factor[0][:, lo:hi] if i == 4 else damp[:, g, c0 + lo:c0 + hi]
+            nc.scalar.activation(dst, roots[i][:, lo:hi], ACT.Square)
 
         for n0 in range(0, S, TOK):
             square_b(0, n0)
@@ -199,19 +204,24 @@ def tile_list_damped_grasp_scores_kernel(tc, tab_words, tab_scales, tab2_words, 
                 grouped = tail.tile([P, PACK, P, PACK], BF16, name="grouped10", align_bytes=64, offset=0)
             else:
                 grouped = held([P, PACK, P, PACK], BF16, "grouped%d%d" % (g, a))
-            dst = grouped[:].rearrange("p t m j -> p m t j")
+            paired = grouped[:].rearrange("p (u v) m j -> p u m j v", u=2)
+
+            def in_pairs(raw):
+                return raw[:].rearrange("p j (m u v) -> p u m j v", u=2, v=2)
+
             if (g, a) == (1, 1):
                 for part, (move, lo, hi) in enumerate(((nc.scalar.copy, 0, SHARE), (nc.vector.tensor_copy, SHARE, P))):
-                    move(dst[:, lo:hi], w1_last[part][:].rearrange("p j (m t) -> p m t j", t=PACK))
+                    move(paired[:, :, lo:hi], in_pairs(w1_last[part]))
                 return grouped
-            src = w1_raw[g, a][:].rearrange("p j (m t) -> p m t j", t=PACK)
             if a == 0:
+                dst = grouped[:].rearrange("p t m j -> p m t j")
+                src = w1_raw[g, a][:].rearrange("p j (m t) -> p m t j", t=PACK)
                 for m0 in range(0, ON_GPSIMD if g else P, 32):
                     nc.gpsimd.tensor_scalar(dst[:, m0:m0 + 32], src[:, m0:m0 + 32], 1.0, 0.0, ALU.mult, ALU.add)
                 if g:
-                    nc.scalar.copy(dst[:, ON_GPSIMD:P], src[:, ON_GPSIMD:P])
+                    nc.scalar.copy(paired[:, :, ON_GPSIMD:P], in_pairs(w1_raw[g, a])[:, :, ON_GPSIMD:P])
             else:
-                nc.vector.tensor_copy(dst, src)
+                nc.vector.tensor_copy(paired, in_pairs(w1_raw[g, a]))
             return grouped
 
         def quantize_w1(g, a, grouped):
@@ -253,6 +263,8 @@ def tile_list_damped_grasp_scores_kernel(tc, tab_words, tab_scales, tab2_words, 
         def damped(g, n0):
             cols = slice(n0 * PACK, (n0 + TOK) * PACK)
             factor = first_factors[:, cols] if g == 0 and cols.start < ON_VECTOR else damp[:, g, cols]
+            if g == 1 and cols.start < span:
+                factor = late_factor[0][:, cols]
             nc.vector.tensor_tensor(h_part(g, n0, n0 + TOK).rearrange("p (n t) -> p n t", t=PACK),
                                     a_banks.pop((g, n0))[:].rearrange("p t n -> p n t"),
                                     factor.rearrange("p (n t) -> p n t", t=PACK), ALU.mult)

@@ -24,9 +24,9 @@ GROUPS = H // PASS
 BLOCKS = S // TOK
 BANKS = 4
 LATE = 896
-FIRST = 256
-AHEAD = 768
-SHARE = 80
+FIRST = 128
+AHEAD = 640
+SHARE = 88
 ON_GPSIMD = 96
 ON_VECTOR = 3 * TOK * PACK
 HALF = S // 2
@@ -40,6 +40,7 @@ def tile_list_damped_grasp_scores_kernel(tc, tab_words, tab_scales, tab2_words, 
         early = ctx.enter_context(tc.tile_pool(name="early", bufs=1))
         late = ctx.enter_context(tc.tile_pool(name="late", bufs=1))
         tail = ctx.enter_context(tc.tile_pool(name="tail", bufs=1))
+        mid = ctx.enter_context(tc.tile_pool(name="mid", bufs=1))
         ring = ctx.enter_context(tc.tile_pool(name="ring", bufs=5))
         psum_ab = ctx.enter_context(tc.psum_pool(name="psum_ab", bufs=1))
         psum_by = ctx.enter_context(tc.psum_pool(name="psum_by", bufs=4))
@@ -70,7 +71,7 @@ def tile_list_damped_grasp_scores_kernel(tc, tab_words, tab_scales, tab2_words, 
         def load_w1(g, a):
             rows = w1[a * PASS:(a + 1) * PASS, g * PASS:(g + 1) * PASS]
             if (g, a) == (1, 1):
-                for part, (at, lo, hi) in enumerate(((7168, 0, SHARE), (4096, SHARE, P))):
+                for part, (at, lo, hi) in enumerate(((6656, 0, SHARE), (4096, SHARE, P))):
                     w1_last.append(late.tile([P, PACK, (hi - lo) * PACK], F32, name="w1_last%d" % part, align_bytes=64, offset=at))
                     nc.sync.dma_start(w1_last[part][:], rows[:, lo * PACK:hi * PACK].rearrange("(p j) c -> p j c", j=PACK))
                 return
@@ -115,9 +116,10 @@ def tile_list_damped_grasp_scores_kernel(tc, tab_words, tab_scales, tab2_words, 
                                   w2_scale_raw[:].bitcast(U8)[:, cols].rearrange("p (m t) -> p t m", t=PACK))
         u_scale_rest = early.tile([P, S - AHEAD], U8, name="u_scale_rest", align_bytes=64, offset=0)
         u_rest = early.tile([P, S], U32, name="u_rest", align_bytes=64, offset=S // 2)
-        gather(u_rest, u_window[:].bitcast(U32), list2, FIRST, 2 * FIRST)
-        gather(u_rest, u_window[:].bitcast(U32), list2, 2 * FIRST, S)
+        gather(u_rest, u_window[:].bitcast(U32), list2, FIRST, 3 * FIRST)
+        gather(u_rest, u_window[:].bitcast(U32), list2, 3 * FIRST, AHEAD)
         nc.vector.tensor_copy(u_scale_rest[:], u_scale_window[:].bitcast(U8).indirect(list2[:, AHEAD // 16:S // 16]))
+        gather(u_rest, u_window[:].bitcast(U32), list2, AHEAD, S)
 
         v_scale_picked = held([P, S], U8, "v_scale_picked")
         gather(v_scale_picked, v_scale_window[:].bitcast(U8), list1, 0, S)
@@ -156,34 +158,30 @@ def tile_list_damped_grasp_scores_kernel(tc, tab_words, tab_scales, tab2_words, 
         all_roots = held([P, len(spans) // 2, span], F32, "all_roots")
         roots = [all_roots[:, i, :] for i in range(len(spans) // 2)]
 
-        late_factor = []
-
         def root_of(i, lo=0, hi=span):
             g, c0 = spans[i]
             if g == 1 and lo == 0:
-                root = late.tile([P, span], F32, name="root%d" % i, align_bytes=64, offset=(i % 2) * 11264)
+                root = late.tile([P, span], F32, name="root%d" % i, align_bytes=64, offset=(0, 10752, 6656, 10752)[i % 4])
                 roots.append(root[:])
             nc.scalar.activation(roots[i][:, lo:hi], damp[:, g, c0 + lo:c0 + hi], ACT.Abs_reciprocal_sqrt, bias=seed[:, 8:9])
 
         def square_root(i, lo=0, hi=span):
             g, c0 = spans[i]
-            if i == 4:
-                late_factor.append(late.tile([P, span], F32, name="factor4", align_bytes=64, offset=7168))
-            dst = late_factor[0][:, lo:hi] if i == 4 else damp[:, g, c0 + lo:c0 + hi]
-            nc.scalar.activation(dst, roots[i][:, lo:hi], ACT.Square)
+            nc.scalar.activation(damp[:, g, c0 + lo:c0 + hi], roots[i][:, lo:hi], ACT.Square)
 
-        for n0 in range(0, S, TOK):
+        for g in range(GROUPS):
+            square_b(g, 0)
+        for n0 in range(TOK, S, TOK):
             square_b(0, n0)
-        for i in (0, 1):
+        for i in (0, 1, 2):
             root_of(i)
-        square_root(1, span // 2, span)
-        for n0 in range(0, S // 2, TOK):
+        for n0 in range(TOK, S // 2, TOK):
             square_b(1, n0)
         later = [multiply_b(1, n0) for n0 in range(S // 2, S, TOK)]
-        for i in (2, 3):
-            root_of(i)
-            square_root(i, 0, span // 2)
-            square_root(i, span // 2, span)
+        root_of(3)
+        square_root(2, span // 2, span)
+        square_root(3, 0, span // 2)
+        square_root(3, span // 2, span)
         for n0, b_bank in zip(range(S // 2, S, TOK), later):
             square_bank(1, n0, b_bank)
 
@@ -202,6 +200,8 @@ def tile_list_damped_grasp_scores_kernel(tc, tab_words, tab_scales, tab2_words, 
         def round_w1(g, a):
             if (g, a) == (1, 0):
                 grouped = tail.tile([P, PACK, P, PACK], BF16, name="grouped10", align_bytes=64, offset=0)
+            elif (g, a) == (0, 1):
+                grouped = mid.tile([P, PACK, P, PACK], BF16, name="grouped01", align_bytes=64, offset=256)
             else:
                 grouped = held([P, PACK, P, PACK], BF16, "grouped%d%d" % (g, a))
             paired = grouped[:].rearrange("p (u v) m j -> p u m j v", u=2)
@@ -262,9 +262,12 @@ def tile_list_damped_grasp_scores_kernel(tc, tab_words, tab_scales, tab2_words, 
 
         def damped(g, n0):
             cols = slice(n0 * PACK, (n0 + TOK) * PACK)
-            factor = first_factors[:, cols] if g == 0 and cols.start < ON_VECTOR else damp[:, g, cols]
-            if g == 1 and cols.start < span:
-                factor = late_factor[0][:, cols]
+            if g == 0 and cols.start < span:
+                factor = first_factors[:, cols]
+            elif g == 0 and cols.start < span + ON_VECTOR:
+                factor = next_factors[:, cols.start - span:cols.stop - span]
+            else:
+                factor = damp[:, g, cols]
             nc.vector.tensor_tensor(h_part(g, n0, n0 + TOK).rearrange("p (n t) -> p n t", t=PACK),
                                     a_banks.pop((g, n0))[:].rearrange("p t n -> p n t"),
                                     factor.rearrange("p (n t) -> p n t", t=PACK), ALU.mult)
@@ -316,15 +319,17 @@ def tile_list_damped_grasp_scores_kernel(tc, tab_words, tab_scales, tab2_words, 
         rounded = [round_w1(0, a) for a in range(K // PASS)]
         for a in range(K // PASS):
             quantize_w1(0, a, rounded[a])
+        first_factors = mid.tile([P, span], F32, name="first_factors", align_bytes=64, offset=512)
+        nc.gpsimd.tensor_tensor(first_factors[:], roots[0], roots[0], ALU.mult)
         load_w1(1, 0)
         load_w1(1, 1)
         gather(v_codes[0], v_window[0][:].bitcast(U32), list1, 0, S)
-        first_factors = held([P, ON_VECTOR], F32, "first_factors", tag="v_window0")
-        first_roots = all_roots[:].rearrange("p i n -> p (i n)")[:, 0:ON_VECTOR]
-        nc.vector.tensor_tensor(first_factors[:], first_roots, first_roots, ALU.mult)
+        next_factors = held([P, ON_VECTOR], F32, "next_factors", tag="v_window0")
+        next_roots = all_roots[:].rearrange("p i n -> p (i n)")[:, span:span + ON_VECTOR]
+        nc.vector.tensor_tensor(next_factors[:], next_roots, next_roots, ALU.mult)
         w3_codes = held([P, GROUPS, N], I32, "w3_codes", tag="v_scale_picked")
         nc.sync.dma_start(w3_codes[:], w3_words.rearrange("a p n t -> p a (n t)").bitcast(I32))
-        w3_scale = held([P, GROUPS, N // 4], I32, "w3_scale", tag="grouped01")
+        w3_scale = mid.tile([P, GROUPS, N // 4], I32, name="w3_scale", align_bytes=64, offset=0)
         nc.gpsimd.memset(w3_scale[:], 0)
         for q in range(4):
             nc.sync.dma_start(w3_scale[q:P:32, :, :],

from contextlib import ExitStack

import concourse.mybir as mybir

K, K2, H, N, T, T2, S = 1024, 512, 1024, 256, 4096, 2048, 1024
FLOPS = 2 * S * (K * H + K2 * H + H * N)

F32 = mybir.dt.float32
BF16 = mybir.dt.bfloat16
I32 = mybir.dt.int32
U32 = mybir.dt.uint32
U16 = mybir.dt.uint16
U8 = mybir.dt.uint8
FP8X4 = mybir.dt.float8_e4m3fn_x4
FP4X4 = mybir.dt.float4_e2m1fn_x4
ACT = mybir.ActivationFunctionType
ALU = mybir.AluOpType

P = 128
PACK = 4
PASS = P * PACK
TOK = 128
GROUPS = H // PASS
BLOCKS = S // TOK
BANKS = 4
LATE = 896
FIRST = 128
AHEAD = 640
SHARE = 88
ON_GPSIMD = 96
ON_VECTOR = 3 * TOK * PACK
HALF = S // 2


def tile_list_damped_grasp_scores_kernel(tc, tab_words, tab_scales, tab2_words, tab2_scales, offs, offs2, w1,
                                                  w2_words, w2_scales, w3_words, w3_scales, bias, out):
    nc = tc.nc
    with ExitStack() as ctx:
        keep = ctx.enter_context(tc.tile_pool(name="keep", bufs=1))
        early = ctx.enter_context(tc.tile_pool(name="early", bufs=1))
        late = ctx.enter_context(tc.tile_pool(name="late", bufs=1))
        tail = ctx.enter_context(tc.tile_pool(name="tail", bufs=1))
        mid = ctx.enter_context(tc.tile_pool(name="mid", bufs=1))
        ring = ctx.enter_context(tc.tile_pool(name="ring", bufs=5))
        psum_ab = ctx.enter_context(tc.psum_pool(name="psum_ab", bufs=1))
        psum_by = ctx.enter_context(tc.psum_pool(name="psum_by", bufs=4))

        def held(shape, dtype, name, tag=None):
            return keep.tile(shape, dtype, name=name, tag=tag or name, align_bytes=64)

        list1 = keep.tile([P, S // 16], U16, name="list1")
        list2 = keep.tile([P, S // 16], U16, name="list2")
        v_window = [held([P, T], I32, "v_window0")]
        v_scale_window = tail.tile([P, T // 4], I32, name="v_scale_window", align_bytes=64, offset=0)
        v_scale = [held([P, S // 4], I32, "v_scale%d" % a) for a in range(K // PASS)]
        u_window = held([P, T2], I32, "u_window")
        u_scale_window = held([P, T2 // 4], I32, "u_scale_window")
        w2_raw = held([P, H // 2], I32, "w2_raw")
        w2_scale_raw = early.tile([P, H // 4], I32, name="w2_scale_raw", align_bytes=64, offset=0)
        w1_raw = {}
        w1_last = []

        seed = held([P, 16], F32, "seed")
        nc.gpsimd.memset(u_scale_window[:], 0)
        nc.gpsimd.memset(w2_scale_raw[:], 0)
        nc.vector.memset(seed[:, 0:1], 1.0)
        nc.vector.memset(v_scale_window[:], 0)
        for plane in v_scale:
            nc.vector.memset(plane[:], 0)

        def load_w1(g, a):
            rows = w1[a * PASS:(a + 1) * PASS, g * PASS:(g + 1) * PASS]
            if (g, a) == (1, 1):
                for part, (at, lo, hi) in enumerate(((6656, 0, SHARE), (4096, SHARE, P))):
                    w1_last.append(late.tile([P, PACK, (hi - lo) * PACK], F32, name="w1_last%d" % part, align_bytes=64, offset=at))
                    nc.sync.dma_start(w1_last[part][:], rows[:, lo * PACK:hi * PACK].rearrange("(p j) c -> p j c", j=PACK))
                return
            if a == 1:
                w1_raw[g, a] = late.tile([P, PACK, PASS], F32, name="w1_raw01", align_bytes=64, offset=4096)
            else:
                w1_raw[g, a] = held([P, PACK, PASS], F32, "w1_raw%d%d" % (g, a), tag="w1_raw%d" % a)
            nc.sync.dma_start(w1_raw[g, a][:], rows.rearrange("(p j) c -> p j c", j=PACK))

        def words_of(packed):
            return packed.rearrange("p n t -> p (n t)").bitcast(I32)

        nc.sync.dma_start(list2[:], offs2)
        for q in range(4):
            nc.sync.dma_start(u_scale_window[q:P:32, :], tab2_scales[0, q:16:4, :].bitcast(I32))
        nc.sync.dma_start(w2_raw[:], w2_words[0].bitcast(I32))
        nc.sync.dma_start(u_window[:], words_of(tab2_words[0]))
        for q in range(4):
            nc.sync.dma_start(w2_scale_raw[q:P:32, :], w2_scales[0, q:16:4, :].bitcast(I32))
        nc.scalar.activation(seed[:, 1:2], seed[:, 0:1], ACT.Abs_reciprocal_sqrt)
        nc.scalar.activation(seed[:, 8:9], seed[:, 1:2], ACT.Sign)
        nc.sync.dma_start(v_scale_window[0:P:4, :], tab_scales.rearrange("a q n -> (a q) n").bitcast(I32))
        nc.sync.dma_start(list1[:], offs)
        for a in range(K // PASS):
            load_w1(0, a)
        nc.sync.dma_start(v_window[0][:], words_of(tab_words[0]))

        def gather(dst, window, offsets, lo, hi):
            nc.vector.tensor_copy(dst[:, lo:hi], window.indirect(offsets[:, lo // 16:hi // 16]))

        w2_codes = held([P, 2 * H], U8, "w2_codes")
        w2_scale = held([P, H], U8, "w2_scale")
        u_scale_first = held([P, AHEAD], U8, "u_scale_first")
        gather(u_scale_first, u_scale_window[:].bitcast(U8), list2, 0, AHEAD)
        nc.vector.tensor_copy(w2_codes[:].bitcast(U16).rearrange("p (g t m) -> p g t m", g=GROUPS, t=PACK),
                              w2_raw[:].bitcast(U16).rearrange("p (g m t) -> p g t m", g=GROUPS, t=PACK))
        u_first = held([P, FIRST], U32, "u_first")
        gather(u_first, u_window[:].bitcast(U32), list2, 0, FIRST)
        for g in range(GROUPS):
            cols = slice(g * PASS, (g + 1) * PASS)
            nc.vector.tensor_copy(w2_scale[:, cols].rearrange("p (t m) -> p t m", t=PACK),
                                  w2_scale_raw[:].bitcast(U8)[:, cols].rearrange("p (m t) -> p t m", t=PACK))
        u_scale_rest = early.tile([P, S - AHEAD], U8, name="u_scale_rest", align_bytes=64, offset=0)
        u_rest = early.tile([P, S], U32, name="u_rest", align_bytes=64, offset=S // 2)
        gather(u_rest, u_window[:].bitcast(U32), list2, FIRST, 3 * FIRST)
        gather(u_rest, u_window[:].bitcast(U32), list2, 3 * FIRST, AHEAD)
        nc.vector.tensor_copy(u_scale_rest[:], u_scale_window[:].bitcast(U8).indirect(list2[:, AHEAD // 16:S // 16]))
        gather(u_rest, u_window[:].bitcast(U32), list2, AHEAD, S)

        v_scale_picked = held([P, S], U8, "v_scale_picked")
        gather(v_scale_picked, v_scale_window[:].bitcast(U8), list1, 0, S)

        def place_scale_rows(a):
            for r in range(4):
                first = 64 * a + 4 * r
                nc.sync.dma_start(v_scale[a][r:P:32, :], v_scale_picked[:].bitcast(I32)[first:first + 49:16, :])

        place_scale_rows(0)
        v_window.append(tail.tile([P, T], I32, name="v_window1", align_bytes=64, offset=0))
        nc.sync.dma_start(v_window[1][:], words_of(tab_words[1]))
        place_scale_rows(1)

        damp = held([P, GROUPS, S * PACK], F32, "damp")

        def multiply_b(g, n0):
            cols = slice(n0, n0 + TOK)
            b_bank = psum_by.tile([P, PACK, TOK], F32, name="b_bank", tag="bank")
            for t in range(PACK):
                m0 = g * PASS + t * P
                nc.tensor.matmul_mx(out=b_bank[:, t, :], lhsT=w2_codes[:, 2 * m0:2 * (m0 + P)].bitcast(FP4X4),
                                    lhsT_scale=w2_scale[:, m0:m0 + P], rhs=(u_first if n0 < FIRST else u_rest)[:, cols].bitcast(FP8X4),
                                    rhs_scale=u_scale_first[:, cols] if n0 < AHEAD else u_scale_rest[:, n0 - AHEAD:n0 - AHEAD + TOK], start=True, stop=True)
            return b_bank

        def square_b(g, n0):
            square_bank(g, n0, multiply_b(g, n0))

        def square_bank(g, n0, b_bank):
            nc.scalar.activation(damp[:, g, n0 * PACK:(n0 + TOK) * PACK].rearrange("p (n t) -> p n t", t=PACK),
                                 b_bank[:].rearrange("p t n -> p n t"), ACT.Square)

        span = 2 * TOK * PACK
        spans = [(g, i * span) for g in range(GROUPS) for i in range(BLOCKS // 2)]
        all_roots = held([P, len(spans) // 2, span], F32, "all_roots")
        roots = [all_roots[:, i, :] for i in range(len(spans) // 2)]

        def root_of(i, lo=0, hi=span):
            g, c0 = spans[i]
            if g == 1 and lo == 0:
                root = late.tile([P, span], F32, name="root%d" % i, align_bytes=64, offset=(0, 10752, 6656, 10752)[i % 4])
                roots.append(root[:])
            nc.scalar.activation(roots[i][:, lo:hi], damp[:, g, c0 + lo:c0 + hi], ACT.Abs_reciprocal_sqrt, bias=seed[:, 8:9])

        def square_root(i, lo=0, hi=span):
            g, c0 = spans[i]
            nc.scalar.activation(damp[:, g, c0 + lo:c0 + hi], roots[i][:, lo:hi], ACT.Square)

        for g in range(GROUPS):
            square_b(g, 0)
        for n0 in range(TOK, S, TOK):
            square_b(0, n0)
        for i in (0, 1, 2):
            root_of(i)
        for n0 in range(TOK, S // 2, TOK):
            square_b(1, n0)
        later = [multiply_b(1, n0) for n0 in range(S // 2, S, TOK)]
        root_of(3)
        square_root(2, span // 2, span)
        square_root(3, 0, span // 2)
        square_root(3, span // 2, span)
        for n0, b_bank in zip(range(S // 2, S, TOK), later):
            square_bank(1, n0, b_bank)

        def late_factors():
            for step in (root_of, square_root):
                for i in (4, 5):
                    step(i)
            for i in (6, 7):
                for step in (root_of, square_root):
                    step(i, 0, span // 2)
                    step(i, span // 2, span)

        w1_codes = held([P, GROUPS, K // PASS, PASS], U32, "w1_codes")
        w1_scale = held([P, GROUPS, K // PASS, PASS], U8, "w1_scale")

        def round_w1(g, a):
            if (g, a) == (1, 0):
                grouped = tail.tile([P, PACK, P, PACK], BF16, name="grouped10", align_bytes=64, offset=0)
            elif (g, a) == (0, 1):
                grouped = mid.tile([P, PACK, P, PACK], BF16, name="grouped01", align_bytes=64, offset=256)
            else:
                grouped = held([P, PACK, P, PACK], BF16, "grouped%d%d" % (g, a))
            paired = grouped[:].rearrange("p (u v) m j -> p u m j v", u=2)

            def in_pairs(raw):
                return raw[:].rearrange("p j (m u v) -> p u m j v", u=2, v=2)

            if (g, a) == (1, 1):
                for part, (move, lo, hi) in enumerate(((nc.scalar.copy, 0, SHARE), (nc.vector.tensor_copy, SHARE, P))):
                    move(paired[:, :, lo:hi], in_pairs(w1_last[part]))
                return grouped
            if a == 0:
                dst = grouped[:].rearrange("p t m j -> p m t j")
                src = w1_raw[g, a][:].rearrange("p j (m t) -> p m t j", t=PACK)
                for m0 in range(0, ON_GPSIMD if g else P, 32):
                    nc.gpsimd.tensor_scalar(dst[:, m0:m0 + 32], src[:, m0:m0 + 32], 1.0, 0.0, ALU.mult, ALU.add)
                if g:
                    nc.scalar.copy(paired[:, :, ON_GPSIMD:P], in_pairs(w1_raw[g, a])[:, :, ON_GPSIMD:P])
            else:
                nc.vector.tensor_copy(paired, in_pairs(w1_raw[g, a]))
            return grouped

        def quantize_w1(g, a, grouped):
            nc.vector.quantize_mx(out=w1_codes[:, g, a, :].bitcast(FP8X4), scales=w1_scale[:, g, a, :],
                                  in_=grouped[:].rearrange("p t m j -> p (t m j)"))

        v_codes = [held([P, S], U32, "v_codes%d" % a) for a in range(K // PASS)]
        h_codes = {}
        h_codes1 = held([P, S], U32, "h_codes1")
        for half in range(2):
            h_codes[1, half] = h_codes1[:, half * HALF:(half + 1) * HALF]

        def codes_of(g, lo, hi):
            return h_codes[g, lo // HALF][:, lo % HALF:lo % HALF + hi - lo].bitcast(FP8X4)

        h_scale = held([P, GROUPS, S], U8, "h_scale")

        h_bf = held([P, GROUPS, S * PACK], BF16, "h_bf")
        a_banks = {}
        waiting = []
        bank_of = {}
        free = list(reversed(range(BANKS)))

        def project(g, n0, a):
            cols = slice(n0, n0 + TOK)
            if a == 0:
                bank_of[g, n0] = free.pop()
                a_banks[g, n0] = psum_ab.tile([P, PACK, TOK], F32, name="a_bank", tag="bank%d" % bank_of[g, n0])
            for t in range(PACK):
                m_cols = slice(t * P, (t + 1) * P)
                nc.tensor.matmul_mx(out=a_banks[g, n0][:, t, :], lhsT=w1_codes[:, g, a, m_cols].bitcast(FP8X4),
                                    lhsT_scale=w1_scale[:, g, a, m_cols],
                                    rhs=v_codes[a][:, cols].bitcast(FP8X4), rhs_scale=v_scale[a][:].bitcast(U8)[:, cols],
                                    start=(a == 0 and t == 0), stop=(a == 1 and t == PACK - 1))

        def h_part(g, lo, hi):
            return h_bf[:, g, lo * PACK:hi * PACK]

        def damped(g, n0):
            cols = slice(n0 * PACK, (n0 + TOK) * PACK)
            if g == 0 and cols.start < span:
                factor = first_factors[:, cols]
            elif g == 0 and cols.start < span + ON_VECTOR:
                factor = next_factors[:, cols.start - span:cols.stop - span]
            else:
                factor = damp[:, g, cols]
            nc.vector.tensor_tensor(h_part(g, n0, n0 + TOK).rearrange("p (n t) -> p n t", t=PACK),
                                    a_banks.pop((g, n0))[:].rearrange("p t n -> p n t"),
                                    factor.rearrange("p (n t) -> p n t", t=PACK), ALU.mult)
            free.append(bank_of[g, n0])
            ahead = waiting.pop(0) if waiting else None
            if ahead:
                project(*ahead, 0)
                project(*ahead, 1)

        def quantize_h(g, lo, hi):
            nc.vector.quantize_mx(out=codes_of(g, lo, hi), scales=h_scale[:, g, lo:hi], in_=h_part(g, lo, hi))

        def score_pass(y, c, g, lo, hi, start, stop):
            nc.tensor.matmul_mx(out=y, lhsT=w3_codes[:, g, c * P:(c + 1) * P].bitcast(FP8X4),
                                lhsT_scale=w3_scale[:, g, :].bitcast(U8)[:, c * P:(c + 1) * P],
                                rhs=codes_of(g, lo, hi), rhs_scale=h_scale[:, g, lo:hi],
                                start=start, stop=stop)

        y_banks = {}

        def open_scores(lo, hi):
            y_banks[lo] = psum_by.tile([P, N // P, hi - lo], F32, name="y_bank", tag="bank")
            for c in range(N // P):
                score_pass(y_banks[lo][:, c, :], c, 0, lo, hi, c == 0, False)

        def scores(lo, hi):
            y_sb = ring.tile([P, N // P, hi - lo], F32, name="y_sb")
            if hi < S:
                y_bank = y_banks.pop(lo)
                for c in range(N // P):
                    score_pass(y_bank[:, c, :], c, 1, lo, hi, False, c == N // P - 1)
                if hi == LATE:
                    quantize_h(1, LATE, S)
                for c in range(N // P):
                    if hi == LATE:
                        nc.vector.tensor_scalar(y_sb[:, c, :], y_bank[:, c, :], bias_sb[:, c:c + 1], None, ALU.add)
                    else:
                        nc.scalar.activation(y_sb[:, c, :], y_bank[:, c, :], ACT.Identity, bias=bias_sb[:, c:c + 1])
            else:
                y_last = [psum_ab.tile([P, hi - lo], F32, name="y_last%d" % c, tag="bank%d" % free[c]) for c in range(N // P)]
                for g in range(GROUPS):
                    for c in range(N // P):
                        score_pass(y_last[c][:], c, g, lo, hi, g == 0, g == GROUPS - 1)
                nc.vector.tensor_scalar(y_sb[:, 0, :], y_last[0][:], bias_sb[:, 0:1], None, ALU.add)
                nc.scalar.activation(y_sb[:, 1, :], y_last[1][:], ACT.Identity, bias=bias_sb[:, 1:2])
            nc.sync.dma_start(out[:, lo:hi].rearrange("(c p) n -> p c n", p=P), y_sb[:])

        halves = ((0, S // 2), (S // 2, S))
        rounded = [round_w1(0, a) for a in range(K // PASS)]
        for a in range(K // PASS):
            quantize_w1(0, a, rounded[a])
        first_factors = mid.tile([P, span], F32, name="first_factors", align_bytes=64, offset=512)
        nc.gpsimd.tensor_tensor(first_factors[:], roots[0], roots[0], ALU.mult)
        load_w1(1, 0)
        load_w1(1, 1)
        gather(v_codes[0], v_window[0][:].bitcast(U32), list1, 0, S)
        next_factors = held([P, ON_VECTOR], F32, "next_factors", tag="v_window0")
        next_roots = all_roots[:].rearrange("p i n -> p (i n)")[:, span:span + ON_VECTOR]
        nc.vector.tensor_tensor(next_factors[:], next_roots, next_roots, ALU.mult)
        w3_codes = held([P, GROUPS, N], I32, "w3_codes", tag="v_scale_picked")
        nc.sync.dma_start(w3_codes[:], w3_words.rearrange("a p n t -> p a (n t)").bitcast(I32))
        w3_scale = mid.tile([P, GROUPS, N // 4], I32, name="w3_scale", align_bytes=64, offset=0)
        nc.gpsimd.memset(w3_scale[:], 0)
        for q in range(4):
            nc.sync.dma_start(w3_scale[q:P:32, :, :],
                              w3_scales[:, q:16:4, :].rearrange("a r n -> r a n").bitcast(I32))
        bias_sb = held([P, N // P], F32, "bias_sb", tag="u_first")
        with nc.allow_non_contiguous_dma(reason="one bias value to a partition"):
            nc.sync.dma_start(bias_sb[:], bias.rearrange("(c p) -> p c", p=P))
        for n0 in range(0, BANKS * TOK, TOK):
            project(0, n0, 0)
        for lo, hi in halves:
            gather(v_codes[1], v_window[1][:].bitcast(U32), list1, lo, hi)

        for n0 in range(0, BANKS * TOK, TOK):
            project(0, n0, 1)
        waiting.extend((0, n0) for n0 in range(BANKS * TOK, LATE, TOK))
        waiting.extend((None, (0, LATE)))
        rounded = [round_w1(1, 0)]
        for n0 in range(0, S, TOK):
            damped(0, n0)
        quantize_w1(1, 0, rounded[0])
        free.reverse()
        for n0 in range(0, BANKS * TOK, TOK):
            project(1, n0, 0)
        rounded.append(round_w1(1, 1))
        late_factors()
        first_codes = tail.tile([P, HALF], U32, name="h_codes00", align_bytes=64, offset=0)
        h_codes[0, 0] = first_codes[:]
        quantize_h(0, 0, 512)
        open_scores(0, 256)
        open_scores(256, 512)
        quantize_w1(1, 1, rounded[1])
        second_codes = held([P, HALF], U32, "h_codes01", tag="grouped11")
        h_codes[0, 1] = second_codes[:]
        for n0 in range(0, BANKS * TOK, TOK):
            project(1, n0, 1)
        waiting.extend((1, n0) for n0 in range(BANKS * TOK, S, TOK))
        quantize_h(0, 512, 1024)
        open_scores(512, 768)
        open_scores(768, 896)
        damped(1, 0)
        chunks = ((0, 256), (256, 512), (512, 768), (768, 896), (896, 1024))
        done = 128
        for lo, hi in chunks:
            while done < min(hi + TOK, S):
                damped(1, done)
                done += TOK
            if hi < S:
                quantize_h(1, lo, hi)
            scores(lo, hi)
